import numpy as np, ml_dtypes
CORES = [48,51,52,55]
N = 4
import mx_ref
BF = ml_dtypes.bfloat16
def gentries(a):
    return np.ascontiguousarray(a.reshape(8, 16, -1).transpose(0, 2, 1)).reshape(8, -1)
def gtable(e):
    e = np.asarray(e); return np.ascontiguousarray(e.reshape(8, -1, 16).transpose(0, 2, 1)).reshape(128, -1).astype(np.int32)
def gcols(t, e):
    v = np.concatenate([t.reshape(8, 16, -1, 4), np.zeros((8, 16, 1, 4), BF)], axis=2)
    return np.ascontiguousarray(np.stack([v[g][:, e[g]] for g in range(8)])).reshape(128, -1)
def tile(rs):
    return np.stack(rs, axis=2).reshape(128, -1).astype(BF)
def pick(q, e):
    c = np.concatenate([q[0].reshape(128, -1, 4), np.zeros((128, 1, 4), np.uint8)], axis=1); s = np.concatenate([q[1], np.ones((16, 1), np.uint8)], axis=1)
    return (np.ascontiguousarray(c[:, e].reshape(128, -1)), np.ascontiguousarray(s[:, e]))
def join(*qs):
    return (np.concatenate([q[0] for q in qs], axis=1), np.concatenate([q[1] for q in qs], axis=1))
def put(q, e, v):
    c, s = q[0].reshape(128, -1, 4).copy(), q[1].copy(); c[:, e] = v[0].reshape(128, -1, 4); s[:, e] = v[1]
    return (c.reshape(128, -1), s)
def pk(c, s):
    return (np.ascontiguousarray(c), mx_ref.live(s))
def emit(q):
    return q[0], q[1]
def packed(v, rng):
    q = [mx_ref.quantize(np.ascontiguousarray(v[r])) for r in range(N)]
    return np.stack([a for a, b in q]), np.stack([mx_ref.plane(b, rng) for a, b in q])
def values_of_codes():
    e, c = np.zeros((128, 128, 4), np.float32), np.zeros((128, 2, 4), np.uint8)
    e[np.arange(128), np.arange(128), 0] = 1
    c[:127, :, 0] = np.arange(256).reshape(2, 128).T[:127]
    return mx_ref.matmul(mx_ref.quantize(e.reshape(128, 512).astype(BF)), (c.reshape(128, 8), np.full((16, 2), 127, np.uint8))).T.reshape(-1).astype(np.float64)
CODE_VALUE, SCALE_VALUE = values_of_codes(), 2.0 ** (np.arange(256) - 127.0)
def decode(q):
    return (CODE_VALUE[q[0]].reshape(16, 8, -1, 4) * SCALE_VALUE[q[1]][:, None, :, None] + 0.0).reshape(128, -1).astype(np.float32)
def f(rng, *shape):
    return mx_ref.flush((rng.standard_normal(shape, dtype=np.float32) * np.exp2(rng.integers(-2, 3, shape[:-1] + (1,)))).astype(BF))
def wide(rng, *shape, cols=0):
    v = rng.standard_normal(shape, dtype=np.float32) * np.exp2(rng.integers(-12, 13, shape)).astype(np.float32)
    if cols: v *= np.repeat(np.exp2(rng.integers(-cols, cols + 1, shape[:-2] + (1, shape[-1] // 4))) * (rng.random(shape[:-2] + (1, shape[-1] // 4)) > 0.0625), 4, axis=-1).astype(np.float32)
    return mx_ref.flush(v.astype(BF))
C, HALF = 448, 224
STEP = [1, 2, 3]
def big(v):
    v = v.astype(np.float32)
    v[np.abs(v) < np.float32(2.0 ** -16)] = 0
    return v.astype(BF)
def numbers_of(rng):
    return {"x": big(f(rng, N, 128, 4 * C)), "u": np.array(f(rng, N, 128, 512)), "v": np.array(f(rng, N, 128, 512))}
def lists(rng):
    e = np.tile(np.arange(C), (N, 8, 1))
    o = rng.permuted(e, axis=2)
    m = np.zeros((N, 8, C), np.int64)
    np.put_along_axis(m, o, o[:, :, np.arange(C) ^ 1], axis=2)
    return rng.permuted(e, axis=2), m
def stored(q, m):
    return {"gq": np.stack([gtable(q[r]) for r in range(N)]), "gm": np.stack([gtable(m[r]) for r in range(N)])}
def layers(rng):
    return big(f(rng, N, 128, 2048)).reshape(N, 8, 16, 4, 8, 16, 4)
def no_layers():
    return np.zeros((N, 8, 16, 4, 8, 16, 4), np.float32)
def weights(rng, w):
    c, p = packed(np.ascontiguousarray(w.astype(BF)).reshape(N, 128, 2048), rng)
    return {"wc": c, "ws": p}
def setup_inputs(rng):
    return {**numbers_of(rng), **stored(*lists(rng)), **weights(rng, layers(rng))}
def setup_inputs_ties(rng):
    d = numbers_of(rng)
    o = rng.permutation(N)
    q, m = lists(rng)
    k = rng.integers(-1, 2, (N, 8, C)).astype(np.float32)
    k[o[0], rng.permutation(8)[:4]] = 0
    k[o[1]] = np.where(rng.permutation(8) < 4, 1, -1)[:, None]
    k[o[3]] = np.where(np.arange(C) < HALF, 1, -3)
    for g in range(8):
        a, b, p = rng.permutation(HALF), HALF + rng.permutation(HALF), rng.permutation(HALF)
        q[o[3], g] = np.concatenate([a, b] if g == 0 else [b, a])
        m[o[3], g, :HALF] = HALF + p
        m[o[3], g, HALF + p] = np.arange(HALF)
    x = d["x"].reshape(N, 8, 16, C, 4)
    x[:, :, 0] = 0
    x[:, :, 0, :, 0] = k.astype(BF)
    u = d["u"].reshape(N, 128, 128, 4)
    u[:, :, ::16] = 0
    for h in range(0, 128, 16): u[:, h, h, 0] = 1
    w = layers(rng)
    w[:, :, :, :, :, 0] = 0
    return {"x": x.reshape(N, 128, 4 * C), "u": u.reshape(N, 128, 512), "v": d["v"], **stored(q, m), **weights(rng, w)}
def setup_inputs_near(rng):
    d = numbers_of(rng)
    o = rng.permutation(N) % 2
    k = np.where(o == 0, 2.0 ** -30, 1.0)
    x = np.zeros((N, 8, 16, C, 4))
    s = rng.integers(-1, 2, (N, 8, C)) * k[:, None, None]
    x[:, :, 0, :, 0] = 1.125 * s
    x[:, :, 1, :, 0] = -1.25 * s
    x[:, :, 7, :, 0] = 2.0 ** -30
    x[:, :, 8, :, 0] = 2.0 ** -30
    for r in range(N):
        at = [0, C - 1, int(rng.integers(C)), int(rng.integers(C))]
        for g, j in zip(rng.permutation(8)[:4], at): x[r, g, 0, j, 0] = 2.0 ** 30 * rng.choice([-1.0, 1.0])
    u = d["u"].reshape(N, 128, 128, 4)
    u[:, :, ::16] = 0
    for h in range(0, 128, 16):
        u[:, h, h, 0] = (1.125 * k).astype(np.float32).astype(BF)
        u[:, h + 1, h, 0] = k.astype(np.float32).astype(BF)
        u[:, h + 9, h, 0] = 2.0 ** -30
    w = no_layers()
    for g in range(8):
        w[:, g, 8, 0, g, 8, 0] = 32
        w[:, g, 1, 0, g, 9, 0] = np.where(o == 0, 2.0 ** -9, 2.0 ** -30)
    return {"x": x.astype(np.float32).reshape(N, 128, 4 * C).astype(BF), "u": u.reshape(N, 128, 512), "v": d["v"], **stored(*lists(rng)), **weights(rng, w)}
def setup_inputs_odd(rng):
    d = numbers_of(rng)
    x = (1.0 + (2 * rng.integers(0, 64, (N, 8, 16, C, 4)) + 1) * 2.0 ** -7) * np.exp2(-rng.integers(0, 7, (N, 8, 16, C, 4)).astype(np.float64)) * rng.choice([-1.0, 1.0], (N, 8, 16, C, 4))
    e = rng.choice([-1.0, 1.0], (N, 8, C)) * 2.0 ** -8
    n = rng.integers(0, 2, (N, 8, C))
    x[:, :, 8:] = 0
    x[:, :, 0, :, 0] = 1.96875 * 2.0 ** 8 * rng.choice([-1.0, 1.0], (N, 8, 1))
    x[:, :, 1, :, 0] = np.where(n == 0, 5.0, 7.0) * e
    x[:, :, 8, :, 0] = np.where(n == 0, -4.5, -7.5) * e
    x[:, :, 10, :, 0] = 1.125 * 2.0 ** -2
    u = d["u"].reshape(N, 128, 128, 4)
    u[:, :, ::16] = 0
    for h in range(0, 128, 16):
        u[:, h + 1, h, 0] = 1
        u[:, h + 8, h, 0] = 1
    w = no_layers()
    for g in range(8):
        w[:, g, 10, 0, g, 9, 0] = 1.75 * 2.0 ** 5
        for b in range(4): w[:, g, 10, b, g, 11:, 0] = rng.choice([1.125, 1.5, 2.0], (N, 5)) * 2.0 ** -9
    return {"x": x.astype(np.float32).reshape(N, 128, 4 * C).astype(BF), "u": u.reshape(N, 128, 512), "v": d["v"], **stored(*lists(rng)), **weights(rng, w)}
def setup_inputs_ends(rng):
    d = numbers_of(rng)
    o, e, h = rng.permutation(N) % 4, rng.permutation(N) % 4, rng.permutation(8)
    s = rng.choice([-1.0, 1.0], (N, 128, C, 4))
    s[o == 0] = -1
    s[o == 1] = rng.choice([-1.0, 1.0], (N, 1, C, 1))[o == 1]
    x = s * (0.955 + 0.02 * rng.random((N, 128, C, 4))) * 2.0 ** 30
    x[o == 3] = 2.0 ** -30
    size = np.where(o == 3, 2.0 ** -30, 2.0 ** 30)
    a = np.stack([rng.permutation(8) % 2 * 2.0 - 1.0 for r in range(N)]) * size[:, None]
    u = d["u"].reshape(N, 128, 128, 4)
    u[:, :, ::16] = a.astype(np.float32).astype(BF)[:, None, :, None]
    v = rng.choice([-1.0, 1.0], (N, 128, 512)) * np.where(o % 2 == 0, 2.0 ** 30, 2.0 ** -30)[:, None, None]
    q, m = lists(rng)
    c = np.arange(C)
    q[e == 0], m[e == 0] = c, C - 1 - c
    q[e == 1], m[e == 1] = C - 1 - c, c ^ 1
    q[e == 2], m[e == 2] = (c + 1) % C, (c + HALF) % C
    w = no_layers()
    i = np.arange(16)
    for r in range(N):
        for b in range(4):
            if o[r] < 3:
                for g in h[:3]: w[r, g, i, b, g, i, b] = -0.125
            w[r, h[4], i, b, h[3], i, b] = 2.0 ** 30 if o[r] == 3 else 2.0 ** -30
    return {"x": x.astype(np.float32).reshape(N, 128, 4 * C).astype(BF), "u": u.reshape(N, 128, 512), "v": v.astype(np.float32).astype(BF), **stored(q, m), **weights(rng, w)}
def setup_inputs_spread(rng):
    d = setup_inputs(rng)
    d["x"] = big(wide(rng, N, 128, 4 * C, cols=6))
    return d
def check_inputs(d):
    b = []
    for k in ("x", "u", "v"):
        a = np.abs(d[k].astype(np.float32))
        if not (np.isfinite(a).all() and ((a == 0) | (a >= 2.0 ** -30) & (a <= 2.0 ** 30)).all()): b.append("a value of " + k)
    none, least, most = [emit(mx_ref.quantize(np.full((128, 16), k, np.float32).astype(BF)))[1][0, 0] for k in (0.0, 2.0 ** -30, 2.0 ** 30)]
    c = np.arange(C)
    for r in range(N):
        if not (np.sort(gentries(d["gq"][r]), axis=1) == c).all(): b.append("gq: not each column once in a group")
        m = gentries(d["gm"][r])
        if not ((m >= 0) & (m < C)).all(): b.append("an entry of gm")
        elif not ((np.take_along_axis(m, m, axis=1) == c) & (m != c)).all(): b.append("gm: not pairs")
        if ((d["wc"][r] == 0x7F) | (d["wc"][r] == 0xFF)).any(): b.append("wc: a code that is no number")
        s = mx_ref.live(d["ws"][r])
        if ((s != none) & ((s < least) | (s > most))).any(): b.append("ws: a scale out of range")
        if (((d["wc"][r].reshape(16, 8, 512, 4) & 0x7F) != 0) & (s == none)[:, None, :, None]).any(): b.append("wc: a code other than zero under the scale of zeros")
    return b
def exchange(s, m):
    bit = np.roll(s[::16] > 0, 1, axis=0)
    return np.where(np.take_along_axis(bit, np.minimum(m, np.arange(C)), axis=1), m, np.arange(C))
def reference(x, u, v, gq, gm, wc, ws):
    qu = [mx_ref.quantize(u[r]) for r in range(N)]
    lay = [pk(wc[r], ws[r]) for r in range(N)]
    kept, pair = [gentries(gq[r]) for r in range(N)], [gentries(gm[r]) for r in range(N)]
    now = [x[r] for r in range(N)]
    for step in STEP:
        mid, back, sent = [], [], []
        for r in range(N):
            q, m = kept[r], pair[r]
            a, b = np.zeros((9, C), np.int64), np.zeros((9, C), np.int64)
            go = exchange(mx_ref.matmul(qu[r], mx_ref.quantize(now[r])), m)
            a[0] = np.arange(C)
            for g in range(8): a[g + 1] = q[g][go[g][a[g]]]
            t = ((now[r].astype(np.float32) + gcols(now[r], a[1:]).astype(np.float32)) * np.float32(0.5)).astype(BF)
            qt = mx_ref.quantize(t)
            go = exchange(mx_ref.matmul(qu[r], qt), m)
            inv = np.argsort(q, axis=1)
            b[8] = a[8]
            for g in range(7, -1, -1): b[g] = go[g][inv[g][b[g + 1]]]
            sent.append(mx_ref.quantize(tile([mx_ref.matmul(pick(lay[r], np.arange(128 * k, 128 * k + 128)), qt) * np.float32(0.03125) for k in range(4)])))
            miss = np.take_along_axis(a[:8] != b[:8], np.minimum(m, np.arange(C)), axis=1)
            kept[r] = np.where(miss, np.take_along_axis(q, m, axis=1), q)
            mid.append(t)
            back.append(b[:8])
        now = [(mid[r].astype(np.float32) + gcols(decode(sent[r ^ step]).astype(BF), back[r]).astype(np.float32)).astype(BF) for r in range(N)]
    y, qo = np.zeros((N, 128, C), np.float32), np.zeros((N, 8, C), np.float32)
    oc, osc = np.zeros((N, 128, 4 * C), np.uint8), np.zeros((N, 16, C), np.uint8)
    for r in range(N):
        q = mx_ref.quantize(now[r])
        y[r] = mx_ref.matmul(mx_ref.quantize(v[r]), q)
        qo[r] = kept[r]
        oc[r], osc[r] = emit(q)
    return {"y": y, "qo": qo, "oc": oc, "osc": osc}

@@ -1,0 +1,401 @@
+from concourse.bass import DstId, RemoteDMATransfer
+from concourse.mybir import dt, AluOpType, ActivationFunctionType
+import comms_topo
+
+STEP = [1, 2, 3]
+C = 448
+CA = 320
+BF, F32, I32, U16, MX, U8 = "bfloat16", "float32", "int32", "uint16", "float8_e4m3fn_x4", "uint8"
+
+SCRATCH = {}
+for _n, _w in (("x0", 1792), ("xt", 1792), ("xh", 1792), ("xg", 1792), ("vt", 1792), ("ht", 1792), ("dd", 1792), ("ut", 512), ("vv", 512),
+               ("wt", 1408), ("eb", 2048), ("zt", 848), ("ident", 128), ("jcol", 128),
+               ("iot", C), ("j16", C), ("j4", C), ("mask16", C), ("mask4", C), ("seg16", C), ("seg4", C), ("masku", 112),
+               ("mf0", C), ("mf1", C), ("mb0", C), ("mb1", C), ("rowq", C), ("rowm", C), ("rowqi", C), ("wA", C), ("wB", C),
+               ("mg", C), ("sc", C), ("sc4", C), ("pu", 112), ("pus", 112), ("ne", C), ("nu", C), ("arow", C), ("sg", C)):
+    SCRATCH[_n] = ("sbuf", [128, _w], BF)
+for _n, _w in (("uc", 128), ("uq", 128), ("vq", 128), ("wq", 512), ("xc", C), ("vc", C), ("ebc", 512), ("shc", 352), ("zc", 212),
+               ("hc0", C), ("hc1", C), ("hc2", C), ("lc0", C), ("lc1", C), ("lc2", C)):
+    SCRATCH[_n] = ("sbuf", [128, _w], MX)
+    SCRATCH[_n + "p"] = ("sbuf", [128, _w], U8)
+for _n, _w in (("qU", 28), ("mU", 28), ("loU", 28), ("qiU", 28), ("loqU", 28), ("lf", 224), ("lb", 224), ("l4", 112), ("p16", 28),
+               ("a8", 28), ("ag", 28), ("ulist", 8), ("qoU", 28)):
+    SCRATCH[_n] = ("sbuf", [128, _w], U16)
+for _n, _w in (("iwb", 224), ("iw", 28), ("qF", 224), ("dF", 224), ("qB", 224), ("dB", 224), ("t1", 112), ("t2", 112), ("t3", 28), ("t4", 28),
+               ("mF", 28), ("t5", 28), ("t6", 28), ("t7", 28), ("t8", 28), ("cp", 1), ("cp16", 1), ("cphi", 1), ("cplo", 1), ("c896", 1), ("ysb", C), ("qrow", C)):
+    SCRATCH[_n] = ("sbuf", [128, _w], F32)
+for _n, _w in (("gqi", 28), ("gmi", 28), ("pi", 1), ("pi1", 1), ("pi2", 1), ("pi3", 1), ("uli", 8), ("uli2", 8)):
+    SCRATCH[_n] = ("sbuf", [128, _w], I32)
+SCRATCH["dl"] = ("dram", [32, 4, 28], U16)
+for _k in range(8):
+    SCRATCH["P%d" % _k] = ("psum", [128, 512], F32)
+SEMAPHORES = ["v", "s", "t", "gc"] + ["d%d" % k for k in range(40)] + ["arr%d" % k for k in range(3)] + ["snt%d" % k for k in range(3)]
+
+
+def rank_program(g, core, T, topo):
+    rank = T.rank_of(core)
+    if rank is None:
+        return
+    A = AluOpType
+    F = ActivationFunctionType
+    queue = {"v": g.vector, "s": g.scalar, "t": g.tensor, "g": g, "y": g.sync}
+    own = {"v": "v", "s": "s", "t": "t", "g": "gc"}
+    known = {q: {} for q in queue}
+    count, W, R, nd = {}, {}, {}, [0]
+
+    def need(q, toks):
+        best = {}
+        for tok in toks:
+            if tok[0] not in best or best[tok[0]][1] < tok[1]:
+                best[tok[0]] = tok
+        order = sorted(best.values(), key=lambda k: -len(k[2]))
+        for sem, val, snap in order:
+            if known[q].get(sem, 0) < val:
+                queue[q].wait_ge(T.sem[sem], val)
+                known[q][sem] = val
+            for k, x in snap.items():
+                if known[q].get(k, 0) < x:
+                    known[q][k] = x
+
+    def deps(reads, writes):
+        toks = []
+        for k in reads:
+            toks += W[k]
+        for k in writes:
+            toks += W.get(k, []) + list(R.get(k, {}).values())
+        return toks
+
+    def done(tok, reads, writes):
+        for k in writes:
+            W[k] = [tok]
+            R[k] = {}
+        for k in reads:
+            if k not in writes:
+                R.setdefault(k, {})[tok[0]] = tok
+
+    def op(q, reads, writes, call):
+        need(q, deps(reads, writes))
+        sem = own[q]
+        count[sem] = count.get(sem, 0) + 1
+        call().then_inc(T.sem[sem], 1)
+        done((sem, count[sem], dict(known[q])), reads, writes)
+
+    def dma(q, pairs, reads, writes):
+        need(q, deps(reads, writes))
+        sem = "d%d" % nd[0]
+        nd[0] += 1
+        for o, i in pairs:
+            queue[q].dma_start(o, i).then_inc(T.sem[sem], 16)
+        count[sem] = 16 * len(pairs)
+        done((sem, count[sem], dict(known[q])), reads, writes)
+
+    def tt(reads, writes, out, a, b, o):
+        op("v", reads, writes, lambda: g.vector.tensor_tensor(out, a, b, o))
+
+    def ts(reads, writes, out, a, s1, o1, s2=None, o2=None):
+        if o2 is None:
+            op("v", reads, writes, lambda: g.vector.tensor_scalar(out, a, s1, None, o1))
+        else:
+            op("v", reads, writes, lambda: g.vector.tensor_scalar(out, a, s1, s2, o1, o2))
+
+    def cp(reads, writes, out, a):
+        op("v", reads, writes, lambda: g.vector.tensor_copy(out, a))
+
+    def fill(writes, out, c):
+        op("v", [], writes, lambda: g.vector.memset(out, c))
+
+    def act(reads, writes, out, a, f=F.Copy, **kw):
+        op("s", reads, writes, lambda: g.scalar.activation(out, a, f, **kw))
+
+    def quant(reads, writes, c, a, b, src, e):
+        op("v", reads, writes, lambda: g.vector.quantize_mx(T[c][:, a:b], T[c + "p"][:, a:b], src[:, e:e + 4 * (b - a)]))
+
+    def mm(reads, writes, out, w, wa, x, xa, n):
+        op("t", reads, writes, lambda: g.tensor.matmul_mx(out, T[w][:, wa:wa + 128], T[w + "p"][:, wa:wa + 128], T[x][:, xa:xa + n], T[x + "p"][:, xa:xa + n], True, True))
+
+    def scan(reads, writes, out, seg, a):
+        op("v", reads, writes, lambda: g.vector.tensor_tensor_scan(out, seg, a, 0.0, A.mult, A.add))
+
+    dma("y", [(T.gqi[:], T.gq[:])], [], ["gqi"])
+    dma("y", [(T.gmi[:], T.gm[:])], [], ["gmi"])
+    dma("y", [(T.ut[:], T.u[:])], [], ["ut"])
+    dma("s", [(T.x0[:, 0:4 * CA], T.x[:, 0:4 * CA])], [], ["x0A"])
+    dma("s", [(T.x0[:, 4 * CA:], T.x[:, 4 * CA:])], [], ["x0B"])
+    dma("s", [(T.wq[:].bitcast(dt.uint8), T.wc[:])], [], ["wqc"])
+    dma("s", [(T.wqp[:], T.ws[:])], [], ["wqp"])
+    dma("y", [(T.vv[:], T.v[:])], [], ["vv"])
+
+    def iota(key, out, pat, base, cm, flag=True):
+        if flag:
+            op("g", [], [key], lambda: g.iota(out, pat, base, cm, allow_small_or_imprecise_dtypes=True))
+        else:
+            op("g", [], [key], lambda: g.iota(out, pat, base, cm))
+    iota("pi", T.pi[:], [[0, 1]], 0, 1, False)
+    iota("uli", T.uli[:], [[16, 8]], -16, 0, False)
+    iota("iot", T.iot[:], [[1, C]], -224, 0)
+    iota("j16", T.j16[:], [[0, 28], [1, 16]], 0, 0)
+    iota("iwb", T.iwb[:], [[0, 8], [16, 28]], 0, 0)
+    iota("jcol", T.jcol[:], [[1, 128]], 0, 0)
+    iota("j4", T.j4[:], [[0, 112], [1, 4]], 0, 0)
+    ts(["pi"], ["pi1"], T.pi1[:], T.pi[:], 15, A.bitwise_and)
+    ts(["pi"], ["pi2"], T.pi2[:], T.pi[:], 2, A.arith_shift_right, 3, A.bitwise_and)
+    ts(["pi"], ["pi3"], T.pi3[:], T.pi[:], 3, A.bitwise_and)
+    ts(["uli"], ["uli2"], T.uli2[:], T.uli[:], 127, A.bitwise_and)
+    cp(["pi"], ["cp"], T.cp[:], T.pi[:])
+    cp(["pi1"], ["cp16"], T.cp16[:], T.pi1[:])
+    cp(["pi2"], ["cphi"], T.cphi[:], T.pi2[:])
+    cp(["pi3"], ["cplo"], T.cplo[:], T.pi3[:])
+    ts(["cplo"], ["c896"], T.c896[:], T.cplo[:], 896.0, A.add)
+    cp(["uli2"], ["ulist"], T.ulist[:], T.uli2[:])
+    fill(["zt"], T.zt[:], 0.0)
+    fill(["wt"], T.wt[:], 0.0)
+    ts(["j16", "cp16"], ["mask16"], T.mask16[:], T.j16[:], T.cp16[:], A.is_equal)
+    ts(["j16"], ["seg16"], T.seg16[:], T.j16[:], 0.0, A.is_gt)
+    ts(["iwb", "cp16"], ["iw"], T.iw[:], T.iwb[:, 0:28], T.cp16[:], A.add)
+    ts(["iwb", "cp16"], ["qF0", "qFr"], T.qF[:], T.iwb[:], T.cp16[:], A.add)
+    fill(["dF0", "dFr"], T.dF[:], 0.0)
+
+    cp(["gqi"], ["qU"], T.qU[:], T.gqi[:])
+    act(["iot", "qU"], ["rowq"], T.rowq[:], T.iot[:, 0:C].indirect(T.qU[:, 0:28]))
+    cp(["gqi"], ["qF0"], T.qF[:, 0:28], T.gqi[:])
+    cp(["gmi"], ["mU"], T.mU[:], T.gmi[:])
+    cp(["gmi"], ["mF"], T.mF[:], T.gmi[:])
+    dma("y", [(T.qF[16 * n:128, 28 * n:28 * n + 28], T.qF[0:128 - 16 * n, 0:28]) for n in range(1, 8)], ["qF0"], ["qFr"])
+    tt(["mF", "iw"], ["t5"], T.t5[:], T.mF[:], T.iw[:], A.min)
+    quant(["ut"], ["uc"], "uc", 0, 128, T.ut, 0)
+    cp(["t5"], ["loU"], T.loU[:], T.t5[:])
+    cp(["uc", "ulist"], ["uqc"], T.uq[:, 0:128].bitcast(dt.uint32), T.uc[:, 0:128].bitcast(dt.uint32).indirect(T.ulist[:, 0:8]))
+    cp(["uc", "ulist"], ["uqs"], T.uqp[:, 0:128], T.ucp[:, 0:128].indirect(T.ulist[:, 0:8]))
+
+    def score(src, key, c, part):
+        a, b, bank = (0, CA, "P0") if part == "A" else (CA, C, "P3")
+        quant([key + part], [c + part], c, a, b, src, 4 * a)
+        mm(["uqc", "uqs", c + part], [bank], T[bank][:, 0:b - a], "uq", 0, c, a, b - a)
+
+    def sign(part):
+        a, b, bank = (0, CA, "P0") if part == "A" else (CA, C, "P3")
+        act([bank], ["sg" + part], T.sg[:, a:b], T[bank][:, 0:b - a], F.Sign, bias=-(2.0 ** -93))
+
+    def halve(src, key, a, b, piece):
+        act([key], ["xh%d" % piece], T.xh[:, a:b], src[:, a:b], F.Copy, scale=0.5)
+
+    XH = ["xh0", "xh1", "xh2"]
+    score(T.x0, "x0", "xc", "A")
+    score(T.x0, "x0", "xc", "B")
+    tt(["rowq", "mU", "mask16"], ["mg"], T.mg[:], T.rowq[:, 0:C].indirect(T.mU[:, 0:28]), T.mask16[:], A.mult)
+    scan(["seg16", "mg"], ["sc"], T.sc[:], T.seg16[:], T.mg[:])
+    ts(["sc"], ["t6"], T.t6[:], T.sc[:, 15:C:16], 224.0, A.add)
+    tt(["t6", "qF0"], ["dF0"], T.dF[:, 0:28], T.t6[:], T.qF[:, 0:28], A.subtract)
+    dma("y", [(T.dF[16 * n:128, 28 * n:28 * n + 28], T.dF[0:128 - 16 * n, 0:28]) for n in range(1, 8)], ["dF0"], ["dFr"])
+    sign("A")
+    sign("B")
+    quant(["zt"], ["zcr"], "zc", 84, 212, T.zt, 336)
+    ts(["jcol", "cp"], ["ident"], T.ident[:], T.jcol[:], T.cp[:], A.is_equal)
+    cp(["ident"], ["wt"], T.wt[:, 448:960:4], T.ident[:])
+    quant(["wt"], ["shc"], "shc", 0, 352, T.wt, 0)
+    halve(T.x0, "x0A", 0, 512, 0)
+    halve(T.x0, "x0A", 512, 4 * CA, 1)
+    halve(T.x0, "x0B", 4 * CA, 4 * C, 2)
+
+    def late_constants():
+        ts(["j4", "cphi"], ["mask4"], T.mask4[:], T.j4[:], T.cphi[:], A.is_equal)
+        ts(["j4"], ["seg4"], T.seg4[:], T.j4[:], 0.0, A.is_gt)
+        ts(["j4", "cplo"], ["masku"], T.masku[:], T.j4[:, 0:112], T.cplo[:], A.is_equal)
+        cp(["iw"], ["ag0", "ag"], T.ag[:], T.iw[:])
+        ts(["iwb", "cp16"], ["qB0", "qBr"], T.qB[:], T.iwb[:], T.cp16[:], A.add)
+        fill(["dB0", "dBr"], T.dB[:], 0.0)
+
+    def back_tables_1():
+        cp(["iot", "qU"], ["rowqi"], T.rowqi[:, 0:C].indirect(T.qU[:, 0:28]), T.iot[:])
+
+    def back_tables_2():
+        tt(["rowqi", "mask16"], ["mg"], T.mg[:], T.rowqi[:], T.mask16[:], A.mult)
+        scan(["seg16", "mg"], ["sc"], T.sc[:], T.seg16[:], T.mg[:])
+        ts(["sc"], ["qiU"], T.qiU[:], T.sc[:, 15:C:16], 224.0, A.add)
+        ts(["sc"], ["qB0"], T.qB[:, 0:28], T.sc[:, 15:C:16], 224.0, A.add)
+        dma("y", [(T.qB[0:128 - 16 * n, 28 * n:28 * n + 28], T.qB[16 * n:128, 0:28]) for n in range(1, 8)], ["qB0"], ["qBr"])
+        tt(["rowm", "qiU", "mask16"], ["mg"], T.mg[:], T.rowm[:, 0:C].indirect(T.qiU[:, 0:28]), T.mask16[:], A.mult)
+        scan(["seg16", "mg"], ["sc"], T.sc[:], T.seg16[:], T.mg[:])
+        ts(["sc"], ["t7"], T.t7[:], T.sc[:, 15:C:16], 224.0, A.add)
+        tt(["t7", "qB0"], ["dB0"], T.dB[:, 0:28], T.t7[:], T.qB[:, 0:28], A.subtract)
+        dma("y", [(T.dB[0:128 - 16 * n, 28 * n:28 * n + 28], T.dB[16 * n:128, 0:28]) for n in range(1, 8)], ["dB0"], ["dBr"])
+        tt(["t7", "qB0"], ["t8"], T.t8[:], T.t7[:], T.qB[:, 0:28], A.min)
+        cp(["t8"], ["loqU"], T.loqU[:], T.t8[:])
+
+    def unpackers():
+        fill(["eb"], T.eb[:], 0.0)
+        for b in range(4):
+            cp(["ident"], ["eb"], T.eb[:, 512 * b + b:512 * b + 512:4], T.ident[:])
+        quant(["eb"], ["ebc"], "ebc", 0, 512, T.eb, 0)
+        quant(["vv"], ["vq"], "vq", 0, 128, T.vv, 0)
+
+    def spread(lo, mask, lst, q, d, way):
+        tt(["sgA", "sgB", lo, mask], ["mg"], T.mg[:], T.sg[:, 0:C].indirect(T[lo][:, 0:28]), T[mask][:], A.mult)
+        scan(["seg16", "mg"], ["sc"], T.sc[:], T.seg16[:], T.mg[:])
+        ts(["sc"], ["zt"], T.zt[:, 336:448:4], T.sc[:, 15:C:16], 0.0, A.is_gt)
+        quant(["zt"], ["zc"], "zc", 0, 128, T.zt, 0)
+        for bank, ns in (("P1", (1, 2, 3)), ("P2", (4, 5, 6, 7))):
+            need("t", deps(["zc", "zcr", "shc"], [bank]))
+            for n in ns:
+                s0, z0 = 112 + way * 16 * n, 84 - 28 * (n - ns[0])
+                i = g.tensor.matmul_mx(T[bank][:, 0:128], T.shc[:, s0:s0 + 128], T.shcp[:, s0:s0 + 128], T.zc[:, z0:z0 + 128], T.zcp[:, z0:z0 + 128], n == ns[0], n == ns[-1])
+            count["t"] = count.get("t", 0) + 1
+            i.then_inc(T.sem["t"], 1)
+            done(("t", count["t"], dict(known["t"])), ["zc", "zcr", "shc"], [bank])
+        tt(["zt", d + "0"], ["t3"], T.t3[:], T.zt[:, 336:448:4], T[d][:, 0:28], A.mult)
+        tt(["t3", q + "0"], ["t4"], T.t4[:], T.t3[:], T[q][:, 0:28], A.add)
+        cp(["t4"], [lst + "o"], T[lst][:, 0:28], T.t4[:])
+
+    def prep(k, part, lst, q, d):
+        bank, a, n = ("P1", 28, 84) if part == "A" else ("P2", 112, 112)
+        if k == 0:
+            tt([bank, d + "r"], ["t1"], T.t1[:, 0:n], T[bank][:, 0:n], T[d][:, a:a + n], A.mult)
+        if k == 1:
+            tt(["t1", q + "r"], ["t2"], T.t2[:, 0:n], T.t1[:, 0:n], T[q][:, a:a + n], A.add)
+        if k == 2:
+            cp(["t2"], [lst + part], T[lst][:, a:a + n], T.t2[:, 0:n])
+
+    def gather(i, lst, nv):
+        src = "iot" if i == 0 else ("wB", "wA")[i % 2]
+        dst = ("wA", "wB")[i % 2]
+        key = ["iot"] if i == 0 else [src + "v", src + "s"]
+        lk = lst + ("o" if i == 0 else "A" if i < 4 else "B")
+        if nv:
+            cp(key + [lk], [dst + "v"] + ([dst + "s"] if nv == 28 else []), T[dst][:, 0:16 * nv], T[src][:, 0:C].indirect(T[lst][:, 28 * i:28 * i + nv]))
+        if nv < 28:
+            act(key + [lk], [dst + "s"] + ([dst + "v"] if nv == 0 else []), T[dst][:, 16 * nv:C], T[src][:, 0:C].indirect(T[lst][:, 28 * i + nv:28 * i + 28]))
+
+    def offsets(src, off, offkeys):
+        tt([src + "v", src + "s", "mask4"] + offkeys, ["mg"], T.mg[:], T[src][:, 0:C].indirect(off), T.mask4[:], A.mult)
+        scan(["seg4", "mg"], ["sc4"], T.sc4[:], T.seg4[:], T.mg[:])
+        ts(["sc4", "c896"], ["l4"], T.l4[:], T.sc4[:, 3:C:4], 4.0, A.mult, T.c896[:], A.add)
+
+    def move(out, okey, win, wkeys, base, bkeys, part):
+        a, b = (0, CA) if part == "A" else (CA, C)
+        tt(wkeys + ["l4"] + bkeys, [okey + part], out[:, 4 * a:4 * b], win[:, 0:4 * C].indirect(T.l4[:, a // 4:b // 4]), base[:, 4 * a:4 * b], A.add)
+
+    mf, mb = "mask16", "mask16"
+    for r in range(3):
+        dst = T.cores[rank ^ STEP[r]]
+        hc, lc = "hc%d" % r, "lc%d" % r
+        dma("y", [(T.xg[:], T.xh[:])], XH, ["xg"])
+        spread("loU", mf, "lf", "qF", "dF", -1)
+        gather(0, "lf", 0 if r == 0 else 4)
+        if r == 0:
+            back_tables_1()
+            late_constants()
+        for k in range(3):
+            prep(k, "A", "lf", "qF", "dF")
+        if r == 0:
+            gather(1, "lf", 0)
+            for k in range(3):
+                prep(k, "B", "lf", "qF", "dF")
+            gather(2, "lf", 0)
+            act(["iot", "mU"], ["rowm"], T.rowm[:], T.iot[:, 0:C].indirect(T.mU[:, 0:28]))
+            gather(3, "lf", 14)
+            back_tables_2()
+            gather(4, "lf", 0)
+            gather(5, "lf", 0)
+            unpackers()
+            gather(6, "lf", 0)
+        else:
+            gather(1, "lf", 10)
+            prep(0, "B", "lf", "qF", "dF")
+            gather(2, "lf", 8)
+            prep(1, "B", "lf", "qF", "dF")
+            gather(3, "lf", 10)
+            prep(2, "B", "lf", "qF", "dF")
+            gather(4, "lf", 0)
+            nxt = "mb%d" % (r % 2)
+            tt(["nu", "loqU", mb], [nxt], T[nxt][:], T.nu[:, 0:C].indirect(T.loqU[:, 0:28]), T[mb][:], A.mult)
+            mb = nxt
+            gather(5, "lf", 14)
+            gather(6, "lf", 14)
+        offsets("wA", T.lf[:, 196:224], ["lfB"])
+        move(T.vt, "vt", T.xh, XH, T.xg, ["xg"], "A")
+        score(T.vt, "vt", "vc", "A")
+        move(T.vt, "vt", T.xh, XH, T.xg, ["xg"], "B")
+        score(T.vt, "vt", "vc", "B")
+        sign("A")
+        sign("B")
+        tt(["sc4", "masku"], ["pu"], T.pu[:], T.sc4[:, 3:C:4], T.masku[:], A.mult)
+        scan(["seg4", "pu"], ["pus"], T.pus[:], T.seg4[:, 0:112], T.pu[:])
+        ts(["pus"], ["p16"], T.p16[:], T.pus[:, 3:112:4], 224.0, A.add)
+        dma("y", [(T.dl[k:32:4, :, :], T.p16[k:128:4, :]) for k in range(4)], ["p16"], ["dl"])
+        dma("y", [(T.a8[16 * k:16 * k + 16, :], T.dl[28:32, :, :]) for k in range(8)], ["dl"], ["a8"])
+        dma("y", [(T.ag[16:128, :], T.dl[0:28, :, :])], ["dl"], ["ag"])
+        for b in range(4):
+            bank = "P%d" % (4 + b)
+            mm(["wqc", "wqp", "vcA", "vcB"], [bank], T[bank][:, 0:C], "wq", 128 * b, "vc", 0, C)
+            act([bank], ["ht%d" % b], T.ht[:, b:4 * C:4], T[bank][:, 0:C], F.Copy, scale=0.03125)
+        spread("loqU", mb, "lb", "qB", "dB", 1)
+        quant(["ht%d" % b for b in range(4)], [hc], hc, 0, C, T.ht, 0)
+        need("g", W[hc])
+        rid, pid, _ = topo.addr(dst)
+        mask, ne = topo.mask(core, dst), len(topo.engines(core, dst))
+        arr, snt = "arr%d" % r, "snt%d" % r
+        g.remote_dma(out_ap=T[lc][:, 0:C].bitcast(dt.uint8), in_ap=T[hc][:, 0:C].bitcast(dt.uint8), remote_sem=T.sem[arr], local_sem=T.sem[snt], pid=pid, routing_id=rid, dma_engine_mask=mask)
+        g.remote_dma(out_ap=T[lc + "p"][:, 0:C], in_ap=T[hc + "p"][:, 0:C], remote_sem=T.sem[arr], local_sem=T.sem[snt], pid=pid, routing_id=rid, dma_engine_mask=mask)
+        count[arr] = count[snt] = 2 * ne
+        W[lc] = [(arr, 2 * ne, {})]
+        gather(0, "lb", 0)
+        for k in range(3):
+            prep(k, "A", "lb", "qB", "dB")
+        gather(1, "lb", 10)
+        prep(0, "B", "lb", "qB", "dB")
+        gather(2, "lb", 8)
+        prep(1, "B", "lb", "qB", "dB")
+        gather(3, "lb", 10)
+        prep(2, "B", "lb", "qB", "dB")
+        gather(4, "lb", 14)
+        gather(5, "lb", 14)
+        gather(6, "lb", 28)
+        gather(7, "lb", 28)
+        for b in range(4):
+            bank = "P%d" % (4 + b)
+            mm(["ebc", lc], [bank], T[bank][:, 0:C], "ebc", 128 * b, lc, 0, C)
+            act([bank], ["dd%d" % b], T.dd[:, b:4 * C:4], T[bank][:, 0:C])
+        act(["iot", "ag0", "ag"], ["arow"], T.arow[:], T.iot[:, 0:C].indirect(T.ag[:, 0:28]))
+        offsets("wB", T.a8[:, 0:28], ["a8"])
+
+        def misses():
+            tt(["wBv", "wBs", "a8", "arow"], ["ne"], T.ne[:], T.wB[:, 0:C].indirect(T.a8[:, 0:28]), T.arow[:], A.not_equal)
+            ts(["ne"], ["nu"], T.nu[:], T.ne[:], -2.0, A.mult, 1.0, A.add)
+
+        def turn(old):
+            new = "mf%d" % (r % 2)
+            tt(["nu", "loU", old], [new], T[new][:], T.nu[:, 0:C].indirect(T.loU[:, 0:28]), T[old][:], A.mult)
+            return new
+        DD = ["dd%d" % b for b in range(4)]
+        if r < 2:
+            move(T.xt, "xt", T.dd, DD, T.vt, ["vtA"], "A")
+            score(T.xt, "xt", "xc", "A")
+            move(T.xt, "xt", T.dd, DD, T.vt, ["vtB"], "B")
+            score(T.xt, "xt", "xc", "B")
+            sign("A")
+            halve(T.xt, "xtA", 0, 512, 0)
+            sign("B")
+            halve(T.xt, "xtA", 512, 4 * CA, 1)
+            halve(T.xt, "xtB", 4 * CA, 4 * C, 2)
+            misses()
+            mf = turn(mf)
+        else:
+            misses()
+            mf = turn(mf)
+            scan(["seg16", mf], ["sc"], T.sc[:], T.seg16[:], T[mf][:])
+            ts(["sc"], ["t3"], T.t3[:], T.sc[:, 15:C:16], 0.0, A.is_lt)
+            tt(["t3", "dF0"], ["t5"], T.t5[:], T.t3[:], T.dF[:, 0:28], A.mult)
+            tt(["t5", "qF0"], ["t6"], T.t6[:], T.t5[:], T.qF[:, 0:28], A.add)
+            cp(["t6"], ["qoU"], T.qoU[:], T.t6[:])
+            act(["iot", "qoU"], ["qrow"], T.qrow[:], T.iot[:, 0:C].indirect(T.qoU[:, 0:28]), F.Identity, bias=224.0)
+            dma("y", [(T.qo[:], T.qrow[0:128:16, :])], ["qrow"], ["qo"])
+            for part, bank, a, b in (("A", "P0", 0, CA), ("B", "P3", CA, C)):
+                move(T.xt, "xt", T.dd, DD, T.vt, ["vt" + part], part)
+                quant(["xt" + part], ["xc" + part], "xc", a, b, T.xt, 4 * a)
+                mm(["vq", "xc" + part], [bank], T[bank][:, 0:b - a], "vq", 0, "xc", a, b - a)
+                act([bank], ["y" + part], T.ysb[:, a:b], T[bank][:, 0:b - a])
+                dma("s", [(T.y[:, a:b], T.ysb[:, a:b])], ["y" + part], ["yo" + part])
+                dma("y", [(T.oc[:, 4 * a:4 * b], T.xc[:, a:b].bitcast(dt.uint8))] + [(T.osc[4 * k:4 * k + 4, a:b], T.xcp[32 * k:32 * k + 4, a:b]) for k in range(4)], ["xc" + part], ["oo" + part])
+    for sem in count:
+        if known["g"].get(sem, 0) < count[sem]:
+            g.wait_ge(T.sem[sem], count[sem])

@@ -12,19 +12,19 @@ for _n, _w in (("x0", 1792), ("xt", 1792), ("xh", 1792), ("xg", 1792), ("vt", 17
                ("wt", 1408), ("eb", 2048), ("zt", 848), ("ident", 128), ("jcol", 128),
                ("iot", C), ("j16", C), ("j4", C), ("mask16", C), ("mask4", C), ("seg16", C), ("seg4", C), ("masku", 112),
                ("mf0", C), ("mf1", C), ("mb0", C), ("mb1", C), ("rowq", C), ("rowm", C), ("rowqi", C), ("wA", C), ("wB", C),
-               ("mg", C), ("sc", C), ("sc4", C), ("pu", 112), ("pus", 112), ("ne", C), ("nu", C), ("arow", C), ("sg", C)):
+               ("mg", C), ("sc", C), ("sc4", C), ("pu", 112), ("pus", 112), ("nu", C), ("sg", C), ("tab", 16), ("pa", 28), ("ag", 28)):
     SCRATCH[_n] = ("sbuf", [128, _w], BF)
 for _n, _w in (("uc", 128), ("uq", 128), ("vq", 128), ("wq", 512), ("xc", C), ("vc", C), ("ebc", 512), ("shc", 352), ("zc", 212),
                ("hc0", C), ("hc1", C), ("hc2", C), ("lc0", C), ("lc1", C), ("lc2", C)):
     SCRATCH[_n] = ("sbuf", [128, _w], MX)
     SCRATCH[_n + "p"] = ("sbuf", [128, _w], U8)
 for _n, _w in (("qU", 28), ("mU", 28), ("loU", 28), ("qiU", 28), ("loqU", 28), ("lf", 224), ("lb", 224), ("l4", 112), ("p16", 28),
-               ("a8", 28), ("ag", 28), ("ulist", 8), ("qoU", 28)):
+               ("a8", 28), ("loP", 28), ("loqP", 28), ("dU", 28), ("ulist", 8), ("qoU", 28)):
     SCRATCH[_n] = ("sbuf", [128, _w], U16)
 for _n, _w in (("iwb", 224), ("iw", 28), ("qF", 224), ("dF", 224), ("qB", 224), ("dB", 224), ("t1", 112), ("t2", 112), ("t3", 28), ("t4", 28),
-               ("mF", 28), ("t5", 28), ("t6", 28), ("t7", 28), ("t8", 28), ("cp", 1), ("cp16", 1), ("cphi", 1), ("cplo", 1), ("c896", 1), ("ysb", C), ("qrow", C)):
+               ("mF", 28), ("t5", 28), ("t6", 28), ("t7", 28), ("t8", 28), ("t9", 28), ("lo", 28), ("loq", 28), ("dhF", 28), ("qhF", 28), ("dhB", 28), ("qhB", 28), ("cp", 1), ("cp16", 1), ("cphi", 1), ("cq", 4), ("ysb", C), ("qrow", C)):
     SCRATCH[_n] = ("sbuf", [128, _w], F32)
-for _n, _w in (("gqi", 28), ("gmi", 28), ("pi", 1), ("pi1", 1), ("pi2", 1), ("pi3", 1), ("uli", 8), ("uli2", 8)):
+for _n, _w in (("gqi", 28), ("gmi", 28), ("li", 84), ("pi", 4), ("uli", 16)):
     SCRATCH[_n] = ("sbuf", [128, _w], I32)
 SCRATCH["dl"] = ("dram", [32, 4, 28], U16)
 for _k in range(8):
@@ -121,36 +121,43 @@ def rank_program(g, core, T, topo):
     dma("y", [(T.ut[:], T.u[:])], [], ["ut"])
     dma("s", [(T.x0[:, 0:4 * CA], T.x[:, 0:4 * CA])], [], ["x0A"])
     dma("s", [(T.x0[:, 4 * CA:], T.x[:, 4 * CA:])], [], ["x0B"])
-    dma("s", [(T.wq[:].bitcast(dt.uint8), T.wc[:])], [], ["wqc"])
-    dma("s", [(T.wqp[:], T.ws[:])], [], ["wqp"])
     dma("y", [(T.vv[:], T.v[:])], [], ["vv"])
+    dma("y", [(T.wq[:].bitcast(dt.uint8), T.wc[:])], [], ["wqc"])
+    dma("y", [(T.wqp[:], T.ws[:])], [], ["wqp"])
 
     def iota(key, out, pat, base, cm, flag=True):
         if flag:
             op("g", [], [key], lambda: g.iota(out, pat, base, cm, allow_small_or_imprecise_dtypes=True))
         else:
             op("g", [], [key], lambda: g.iota(out, pat, base, cm))
-    iota("pi", T.pi[:], [[0, 1]], 0, 1, False)
-    iota("uli", T.uli[:], [[16, 8]], -16, 0, False)
-    iota("iot", T.iot[:], [[1, C]], -224, 0)
+    iota("pi", T.pi[:, 0:1], [[0, 1]], 0, 1, False)
+    iota("uli", T.uli[:, 0:8], [[16, 8]], -16, 0, False)
     iota("j16", T.j16[:], [[0, 28], [1, 16]], 0, 0)
-    iota("iwb", T.iwb[:], [[0, 8], [16, 28]], 0, 0)
     iota("jcol", T.jcol[:], [[1, 128]], 0, 0)
+    iota("iot", T.iot[:], [[1, C]], -224, 0)
+    iota("iwb", T.iwb[:], [[0, 8], [16, 28]], 0, 0)
     iota("j4", T.j4[:], [[0, 112], [1, 4]], 0, 0)
-    ts(["pi"], ["pi1"], T.pi1[:], T.pi[:], 15, A.bitwise_and)
-    ts(["pi"], ["pi2"], T.pi2[:], T.pi[:], 2, A.arith_shift_right, 3, A.bitwise_and)
-    ts(["pi"], ["pi3"], T.pi3[:], T.pi[:], 3, A.bitwise_and)
-    ts(["uli"], ["uli2"], T.uli2[:], T.uli[:], 127, A.bitwise_and)
-    cp(["pi"], ["cp"], T.cp[:], T.pi[:])
-    cp(["pi1"], ["cp16"], T.cp16[:], T.pi1[:])
-    cp(["pi2"], ["cphi"], T.cphi[:], T.pi2[:])
-    cp(["pi3"], ["cplo"], T.cplo[:], T.pi3[:])
-    ts(["cplo"], ["c896"], T.c896[:], T.cplo[:], 896.0, A.add)
-    cp(["uli2"], ["ulist"], T.ulist[:], T.uli2[:])
+    cplo, c896, cpt, cpp = (T.cq[:, k:k + 1] for k in range(4))
+    ts(["pi"], ["pi1"], T.pi[:, 1:2], T.pi[:, 0:1], 15, A.bitwise_and)
+    ts(["pi"], ["pi2"], T.pi[:, 2:3], T.pi[:, 0:1], 2, A.arith_shift_right, 3, A.bitwise_and)
+    ts(["pi"], ["pi3"], T.pi[:, 3:4], T.pi[:, 0:1], 3, A.bitwise_and)
+    ts(["uli"], ["uli2"], T.uli[:, 8:16], T.uli[:, 0:8], 127, A.bitwise_and)
+    cp(["pi"], ["cp"], T.cp[:], T.pi[:, 0:1])
+    cp(["pi1"], ["cp16"], T.cp16[:], T.pi[:, 1:2])
+    cp(["pi2"], ["cphi"], T.cphi[:], T.pi[:, 2:3])
+    cp(["pi3"], ["cplo"], cplo, T.pi[:, 3:4])
+    cp(["uli2"], ["ulist"], T.ulist[:], T.uli[:, 8:16])
+    ts(["cplo"], ["c896"], c896, cplo, 896.0, A.add)
+    ts(["cplo"], ["cpt"], cpt, cplo, 4.0, A.mult, -224.0, A.add)
     fill(["zt"], T.zt[:], 0.0)
     fill(["wt"], T.wt[:], 0.0)
     ts(["j16", "cp16"], ["mask16"], T.mask16[:], T.j16[:], T.cp16[:], A.is_equal)
     ts(["j16"], ["seg16"], T.seg16[:], T.j16[:], 0.0, A.is_gt)
+    ts(["jcol", "cp"], ["ident"], T.ident[:], T.jcol[:], T.cp[:], A.is_equal)
+    ts(["jcol"], ["tab"], T.tab[:], T.jcol[:, 0:16], -2.0, A.mult, 1.0, A.add)
+    cp(["ident"], ["wt"], T.wt[:, 448:960:4], T.ident[:])
+    quant(["wt"], ["shc"], "shc", 0, 352, T.wt, 0)
+    quant(["zt"], ["zcr"], "zc", 84, 212, T.zt, 336)
     ts(["iwb", "cp16"], ["iw"], T.iw[:], T.iwb[:, 0:28], T.cp16[:], A.add)
     ts(["iwb", "cp16"], ["qF0", "qFr"], T.qF[:], T.iwb[:], T.cp16[:], A.add)
     fill(["dF0", "dFr"], T.dF[:], 0.0)
@@ -161,9 +168,18 @@ def rank_program(g, core, T, topo):
     cp(["gmi"], ["mU"], T.mU[:], T.gmi[:])
     cp(["gmi"], ["mF"], T.mF[:], T.gmi[:])
     dma("y", [(T.qF[16 * n:128, 28 * n:28 * n + 28], T.qF[0:128 - 16 * n, 0:28]) for n in range(1, 8)], ["qF0"], ["qFr"])
-    tt(["mF", "iw"], ["t5"], T.t5[:], T.mF[:], T.iw[:], A.min)
+    tt(["mF", "iw"], ["lo"], T.lo[:], T.mF[:], T.iw[:], A.min)
     quant(["ut"], ["uc"], "uc", 0, 128, T.ut, 0)
-    cp(["t5"], ["loU"], T.loU[:], T.t5[:])
+    cp(["lo"], ["loU"], T.loU[:], T.lo[:])
+    tt(["rowq", "mU", "mask16"], ["mg"], T.mg[:], T.rowq[:, 0:C].indirect(T.mU[:, 0:28]), T.mask16[:], A.mult)
+    scan(["seg16", "mg"], ["sc"], T.sc[:], T.seg16[:], T.mg[:])
+    ts(["sc"], ["t6"], T.t6[:], T.sc[:, 15:C:16], 224.0, A.add)
+    tt(["t6", "qF0"], ["dF0"], T.dF[:, 0:28], T.t6[:], T.qF[:, 0:28], A.subtract)
+    dma("y", [(T.dF[16 * n:128, 28 * n:28 * n + 28], T.dF[0:128 - 16 * n, 0:28]) for n in range(1, 8)], ["dF0"], ["dFr"])
+    for a, b in ((0, 848), (848, 1696), (1696, 2048)):
+        act(["zt"], ["eb%d" % a], T.eb[:, a:b], T.zt[:, 0:b - a])
+    for b in range(4):
+        act(["ident", "eb0", "eb848", "eb1696"], ["ebi%d" % b], T.eb[:, 512 * b + b:512 * b + 512:4], T.ident[:])
     cp(["uc", "ulist"], ["uqc"], T.uq[:, 0:128].bitcast(dt.uint32), T.uc[:, 0:128].bitcast(dt.uint32).indirect(T.ulist[:, 0:8]))
     cp(["uc", "ulist"], ["uqs"], T.uqp[:, 0:128], T.ucp[:, 0:128].indirect(T.ulist[:, 0:8]))
 
@@ -182,28 +198,31 @@ def rank_program(g, core, T, topo):
     XH = ["xh0", "xh1", "xh2"]
     score(T.x0, "x0", "xc", "A")
     score(T.x0, "x0", "xc", "B")
-    tt(["rowq", "mU", "mask16"], ["mg"], T.mg[:], T.rowq[:, 0:C].indirect(T.mU[:, 0:28]), T.mask16[:], A.mult)
-    scan(["seg16", "mg"], ["sc"], T.sc[:], T.seg16[:], T.mg[:])
-    ts(["sc"], ["t6"], T.t6[:], T.sc[:, 15:C:16], 224.0, A.add)
-    tt(["t6", "qF0"], ["dF0"], T.dF[:, 0:28], T.t6[:], T.qF[:, 0:28], A.subtract)
-    dma("y", [(T.dF[16 * n:128, 28 * n:28 * n + 28], T.dF[0:128 - 16 * n, 0:28]) for n in range(1, 8)], ["dF0"], ["dFr"])
     sign("A")
     sign("B")
-    quant(["zt"], ["zcr"], "zc", 84, 212, T.zt, 336)
-    ts(["jcol", "cp"], ["ident"], T.ident[:], T.jcol[:], T.cp[:], A.is_equal)
-    cp(["ident"], ["wt"], T.wt[:, 448:960:4], T.ident[:])
-    quant(["wt"], ["shc"], "shc", 0, 352, T.wt, 0)
+    quant(["vv"], ["vq"], "vq", 0, 128, T.vv, 0)
+    ts(["dF0"], ["dhF"], T.dhF[:], T.dF[:, 0:28], 0.5, A.mult)
+    tt(["dhF", "qF0"], ["qhF"], T.qhF[:], T.dhF[:], T.qF[:, 0:28], A.add)
+    quant(["ebi0", "ebi1", "ebi2", "ebi3"], ["ebc"], "ebc", 0, 512, T.eb, 0)
     halve(T.x0, "x0A", 0, 512, 0)
     halve(T.x0, "x0A", 512, 4 * CA, 1)
     halve(T.x0, "x0B", 4 * CA, 4 * C, 2)
+    tt(["cpt", "cphi"], ["cpp"], cpp, cpt, T.cphi[:], A.add)
 
     def late_constants():
         ts(["j4", "cphi"], ["mask4"], T.mask4[:], T.j4[:], T.cphi[:], A.is_equal)
         ts(["j4"], ["seg4"], T.seg4[:], T.j4[:], 0.0, A.is_gt)
-        ts(["j4", "cplo"], ["masku"], T.masku[:], T.j4[:, 0:112], T.cplo[:], A.is_equal)
-        cp(["iw"], ["ag0", "ag"], T.ag[:], T.iw[:])
-        ts(["iwb", "cp16"], ["qB0", "qBr"], T.qB[:], T.iwb[:], T.cp16[:], A.add)
-        fill(["dB0", "dBr"], T.dB[:], 0.0)
+        ts(["j4", "cplo"], ["masku"], T.masku[:], T.j4[:, 0:112], cplo, A.is_equal)
+        ts(["iwb", "cpp"], ["ag0", "ag"], T.ag[:], T.iwb[:, 0:28], cpp, A.add)
+
+    def turned(src, dst):
+        cp([src], ["li"], T.li[:, 0:28], T[src][:])
+        ts(["li"], ["li1"], T.li[:, 28:56], T.li[:, 0:28], 3, A.bitwise_and)
+        ts(["li"], ["li2"], T.li[:, 56:84], T.li[:, 0:28], 2, A.arith_shift_right, 3, A.bitwise_and)
+        tt(["li1", "li2"], ["t9"], T.t9[:], T.li[:, 28:56], T.li[:, 56:84], A.subtract)
+        ts(["t9"], ["t5"], T.t5[:], T.t9[:], 3.0, A.mult)
+        tt(["t5", src], ["t6"], T.t6[:], T.t5[:], T[src][:], A.add)
+        cp(["t6"], [dst], T[dst][:], T.t6[:])
 
     def back_tables_1():
         cp(["iot", "qU"], ["rowqi"], T.rowqi[:, 0:C].indirect(T.qU[:, 0:28]), T.iot[:])
@@ -219,21 +238,20 @@ def rank_program(g, core, T, topo):
         ts(["sc"], ["t7"], T.t7[:], T.sc[:, 15:C:16], 224.0, A.add)
         tt(["t7", "qB0"], ["dB0"], T.dB[:, 0:28], T.t7[:], T.qB[:, 0:28], A.subtract)
         dma("y", [(T.dB[0:128 - 16 * n, 28 * n:28 * n + 28], T.dB[16 * n:128, 0:28]) for n in range(1, 8)], ["dB0"], ["dBr"])
-        tt(["t7", "qB0"], ["t8"], T.t8[:], T.t7[:], T.qB[:, 0:28], A.min)
-        cp(["t8"], ["loqU"], T.loqU[:], T.t8[:])
-
-    def unpackers():
-        fill(["eb"], T.eb[:], 0.0)
-        for b in range(4):
-            cp(["ident"], ["eb"], T.eb[:, 512 * b + b:512 * b + 512:4], T.ident[:])
-        quant(["eb"], ["ebc"], "ebc", 0, 512, T.eb, 0)
-        quant(["vv"], ["vq"], "vq", 0, 128, T.vv, 0)
+        tt(["t7", "qB0"], ["loq"], T.loq[:], T.t7[:], T.qB[:, 0:28], A.min)
+        ts(["dB0"], ["dhB"], T.dhB[:], T.dB[:, 0:28], 0.5, A.mult)
+        cp(["loq"], ["loqU"], T.loqU[:], T.loq[:])
+        tt(["dhB", "qB0"], ["qhB"], T.qhB[:], T.dhB[:], T.qB[:, 0:28], A.add)
 
     def spread(lo, mask, lst, q, d, way):
         tt(["sgA", "sgB", lo, mask], ["mg"], T.mg[:], T.sg[:, 0:C].indirect(T[lo][:, 0:28]), T[mask][:], A.mult)
         scan(["seg16", "mg"], ["sc"], T.sc[:], T.seg16[:], T.mg[:])
+        dh, qh = ("dhF", "qhF") if lst == "lf" else ("dhB", "qhB")
         ts(["sc"], ["zt"], T.zt[:, 336:448:4], T.sc[:, 15:C:16], 0.0, A.is_gt)
+        tt(["sc", dh], ["t3"], T.t3[:], T.sc[:, 15:C:16], T[dh][:], A.mult)
         quant(["zt"], ["zc"], "zc", 0, 128, T.zt, 0)
+        tt(["t3", qh], ["t4"], T.t4[:], T.t3[:], T[qh][:], A.add)
+        cp(["t4"], [lst + "o"], T[lst][:, 0:28], T.t4[:])
         for bank, ns in (("P1", (1, 2, 3)), ("P2", (4, 5, 6, 7))):
             need("t", deps(["zc", "zcr", "shc"], [bank]))
             for n in ns:
@@ -242,9 +260,6 @@ def rank_program(g, core, T, topo):
             count["t"] = count.get("t", 0) + 1
             i.then_inc(T.sem["t"], 1)
             done(("t", count["t"], dict(known["t"])), ["zc", "zcr", "shc"], [bank])
-        tt(["zt", d + "0"], ["t3"], T.t3[:], T.zt[:, 336:448:4], T[d][:, 0:28], A.mult)
-        tt(["t3", q + "0"], ["t4"], T.t4[:], T.t3[:], T[q][:, 0:28], A.add)
-        cp(["t4"], [lst + "o"], T[lst][:, 0:28], T.t4[:])
 
     def prep(k, part, lst, q, d):
         bank, a, n = ("P1", 28, 84) if part == "A" else ("P2", 112, 112)
@@ -268,7 +283,7 @@ def rank_program(g, core, T, topo):
     def offsets(src, off, offkeys):
         tt([src + "v", src + "s", "mask4"] + offkeys, ["mg"], T.mg[:], T[src][:, 0:C].indirect(off), T.mask4[:], A.mult)
         scan(["seg4", "mg"], ["sc4"], T.sc4[:], T.seg4[:], T.mg[:])
-        ts(["sc4", "c896"], ["l4"], T.l4[:], T.sc4[:, 3:C:4], 4.0, A.mult, T.c896[:], A.add)
+        ts(["sc4", "c896"], ["l4"], T.l4[:], T.sc4[:, 3:C:4], 4.0, A.mult, c896, A.add)
 
     def move(out, okey, win, wkeys, base, bkeys, part):
         a, b = (0, CA) if part == "A" else (CA, C)
@@ -281,23 +296,20 @@ def rank_program(g, core, T, topo):
         dma("y", [(T.xg[:], T.xh[:])], XH, ["xg"])
         spread("loU", mf, "lf", "qF", "dF", -1)
         gather(0, "lf", 0 if r == 0 else 4)
-        if r == 0:
-            back_tables_1()
-            late_constants()
         for k in range(3):
             prep(k, "A", "lf", "qF", "dF")
         if r == 0:
-            gather(1, "lf", 0)
             for k in range(3):
                 prep(k, "B", "lf", "qF", "dF")
-            gather(2, "lf", 0)
-            act(["iot", "mU"], ["rowm"], T.rowm[:], T.iot[:, 0:C].indirect(T.mU[:, 0:28]))
-            gather(3, "lf", 14)
+            for k in range(1, 7):
+                gather(k, "lf", 0)
+                if k == 2:
+                    act(["iwb", "cp16"], ["qB0", "qBr"], T.qB[:], T.iwb[:], F.Identity, bias=T.cp16[:])
+                    act(["wt"], ["dB0", "dBr"], T.dB[:], T.wt[:, 0:224])
+                    act(["iot", "mU"], ["rowm"], T.rowm[:], T.iot[:, 0:C].indirect(T.mU[:, 0:28]))
+            late_constants()
+            back_tables_1()
             back_tables_2()
-            gather(4, "lf", 0)
-            gather(5, "lf", 0)
-            unpackers()
-            gather(6, "lf", 0)
         else:
             gather(1, "lf", 10)
             prep(0, "B", "lf", "qF", "dF")
@@ -307,29 +319,39 @@ def rank_program(g, core, T, topo):
             prep(2, "B", "lf", "qF", "dF")
             gather(4, "lf", 0)
             nxt = "mb%d" % (r % 2)
-            tt(["nu", "loqU", mb], [nxt], T[nxt][:], T.nu[:, 0:C].indirect(T.loqU[:, 0:28]), T[mb][:], A.mult)
+            tt(["nu", "loqP", mb], [nxt], T[nxt][:], T.nu[:, 0:C].indirect(T.loqP[:, 0:28]), T[mb][:], A.mult)
             mb = nxt
             gather(5, "lf", 14)
             gather(6, "lf", 14)
         offsets("wA", T.lf[:, 196:224], ["lfB"])
         move(T.vt, "vt", T.xh, XH, T.xg, ["xg"], "A")
         score(T.vt, "vt", "vc", "A")
-        move(T.vt, "vt", T.xh, XH, T.xg, ["xg"], "B")
-        score(T.vt, "vt", "vc", "B")
         sign("A")
+
+        def layer(b, part):
+            a, e = (0, CA) if part == "A" else (CA, C)
+            bank = "P%d" % (4 + b)
+            mm(["wqc", "wqp", "vc" + part], [bank], T[bank][:, 0:e - a], "wq", 128 * b, "vc", a, e - a)
+            act([bank], ["ht%d%s" % (b, part)], T.ht[:, 4 * a + b:4 * e:4], T[bank][:, 0:e - a], F.Copy, scale=0.03125)
+        layer(0, "A")
+        move(T.vt, "vt", T.xh, XH, T.xg, ["xg"], "B")
+        mm(["wqc", "wqp", "vcA"], ["P5"], T.P5[:, 0:CA], "wq", 128, "vc", 0, CA)
+        score(T.vt, "vt", "vc", "B")
         sign("B")
+        act(["P5"], ["ht1A"], T.ht[:, 1:4 * CA:4], T.P5[:, 0:CA], F.Copy, scale=0.03125)
+        layer(2, "A")
+        layer(3, "A")
+        for b in range(4):
+            layer(b, "B")
         tt(["sc4", "masku"], ["pu"], T.pu[:], T.sc4[:, 3:C:4], T.masku[:], A.mult)
         scan(["seg4", "pu"], ["pus"], T.pus[:], T.seg4[:, 0:112], T.pu[:])
         ts(["pus"], ["p16"], T.p16[:], T.pus[:, 3:112:4], 224.0, A.add)
+        cp(["pus"], ["pa"], T.pa[:], T.pus[:, 3:112:4])
         dma("y", [(T.dl[k:32:4, :, :], T.p16[k:128:4, :]) for k in range(4)], ["p16"], ["dl"])
+        dma("y", [(T.ag[16:128, :], T.pa[0:112, :])], ["pa"], ["ag"])
         dma("y", [(T.a8[16 * k:16 * k + 16, :], T.dl[28:32, :, :]) for k in range(8)], ["dl"], ["a8"])
-        dma("y", [(T.ag[16:128, :], T.dl[0:28, :, :])], ["dl"], ["ag"])
-        for b in range(4):
-            bank = "P%d" % (4 + b)
-            mm(["wqc", "wqp", "vcA", "vcB"], [bank], T[bank][:, 0:C], "wq", 128 * b, "vc", 0, C)
-            act([bank], ["ht%d" % b], T.ht[:, b:4 * C:4], T[bank][:, 0:C], F.Copy, scale=0.03125)
         spread("loqU", mb, "lb", "qB", "dB", 1)
-        quant(["ht%d" % b for b in range(4)], [hc], hc, 0, C, T.ht, 0)
+        quant(["ht%d%s" % (b, k) for b in range(4) for k in "AB"], [hc], hc, 0, C, T.ht, 0)
         need("g", W[hc])
         rid, pid, _ = topo.addr(dst)
         mask, ne = topo.mask(core, dst), len(topo.engines(core, dst))
@@ -355,21 +377,30 @@ def rank_program(g, core, T, topo):
             bank = "P%d" % (4 + b)
             mm(["ebc", lc], [bank], T[bank][:, 0:C], "ebc", 128 * b, lc, 0, C)
             act([bank], ["dd%d" % b], T.dd[:, b:4 * C:4], T[bank][:, 0:C])
-        act(["iot", "ag0", "ag"], ["arow"], T.arow[:], T.iot[:, 0:C].indirect(T.ag[:, 0:28]))
         offsets("wB", T.a8[:, 0:28], ["a8"])
+        tt(["sc4", "masku"], ["pu"], T.pu[:], T.sc4[:, 3:C:4], T.masku[:], A.mult)
+        scan(["seg4", "pu"], ["pus"], T.pus[:], T.seg4[:, 0:112], T.pu[:])
+        if r == 0:
+            turned("lo", "loP")
+            turned("loq", "loqP")
 
-        def misses():
-            tt(["wBv", "wBs", "a8", "arow"], ["ne"], T.ne[:], T.wB[:, 0:C].indirect(T.a8[:, 0:28]), T.arow[:], A.not_equal)
-            ts(["ne"], ["nu"], T.nu[:], T.ne[:], -2.0, A.mult, 1.0, A.add)
+        def differ(k):
+            if k == 0:
+                tt(["pus", "ag", "ag0"], ["t8"], T.t8[:], T.pus[:, 3:112:4], T.ag[:], A.subtract)
+            else:
+                ts(["t8"], ["dU"], T.dU[:], T.t8[:], 0.0, A.not_equal)
+                act(["tab", "dU"], ["nu"], T.nu[:], T.tab[:, 0:16].indirect(T.dU[:, 0:28]))
 
         def turn(old):
             new = "mf%d" % (r % 2)
-            tt(["nu", "loU", old], [new], T[new][:], T.nu[:, 0:C].indirect(T.loU[:, 0:28]), T[old][:], A.mult)
+            tt(["nu", "loP", old], [new], T[new][:], T.nu[:, 0:C].indirect(T.loP[:, 0:28]), T[old][:], A.mult)
             return new
         DD = ["dd%d" % b for b in range(4)]
         if r < 2:
             move(T.xt, "xt", T.dd, DD, T.vt, ["vtA"], "A")
+            differ(0)
             score(T.xt, "xt", "xc", "A")
+            differ(1)
             move(T.xt, "xt", T.dd, DD, T.vt, ["vtB"], "B")
             score(T.xt, "xt", "xc", "B")
             sign("A")
@@ -377,20 +408,21 @@ def rank_program(g, core, T, topo):
             sign("B")
             halve(T.xt, "xtA", 512, 4 * CA, 1)
             halve(T.xt, "xtB", 4 * CA, 4 * C, 2)
-            misses()
             mf = turn(mf)
         else:
-            misses()
-            mf = turn(mf)
-            scan(["seg16", mf], ["sc"], T.sc[:], T.seg16[:], T[mf][:])
-            ts(["sc"], ["t3"], T.t3[:], T.sc[:, 15:C:16], 0.0, A.is_lt)
-            tt(["t3", "dF0"], ["t5"], T.t5[:], T.t3[:], T.dF[:, 0:28], A.mult)
-            tt(["t5", "qF0"], ["t6"], T.t6[:], T.t5[:], T.qF[:, 0:28], A.add)
-            cp(["t6"], ["qoU"], T.qoU[:], T.t6[:])
-            act(["iot", "qoU"], ["qrow"], T.qrow[:], T.iot[:, 0:C].indirect(T.qoU[:, 0:28]), F.Identity, bias=224.0)
-            dma("y", [(T.qo[:], T.qrow[0:128:16, :])], ["qrow"], ["qo"])
+            differ(0)
+            differ(1)
             for part, bank, a, b in (("A", "P0", 0, CA), ("B", "P3", CA, C)):
                 move(T.xt, "xt", T.dd, DD, T.vt, ["vt" + part], part)
+                if part == "A":
+                    mf = turn(mf)
+                    scan(["seg16", mf], ["sc"], T.sc[:], T.seg16[:], T[mf][:])
+                    ts(["sc"], ["t3"], T.t3[:], T.sc[:, 15:C:16], 0.0, A.is_lt)
+                    tt(["t3", "dF0"], ["t5"], T.t5[:], T.t3[:], T.dF[:, 0:28], A.mult)
+                    tt(["t5", "qF0"], ["t6"], T.t6[:], T.t5[:], T.qF[:, 0:28], A.add)
+                    cp(["t6"], ["qoU"], T.qoU[:], T.t6[:])
+                    act(["iot", "qoU"], ["qrow"], T.qrow[:], T.iot[:, 0:C].indirect(T.qoU[:, 0:28]), F.Identity, bias=224.0)
+                    dma("y", [(T.qo[:], T.qrow[0:128:16, :])], ["qrow"], ["qo"])
                 quant(["xt" + part], ["xc" + part], "xc", a, b, T.xt, 4 * a)
                 mm(["vq", "xc" + part], [bank], T[bank][:, 0:b - a], "vq", 0, "xc", a, b - a)
                 act([bank], ["y" + part], T.ysb[:, a:b], T[bank][:, 0:b - a])

from concourse.bass import DstId, RemoteDMATransfer
from concourse.mybir import dt, AluOpType, ActivationFunctionType
import comms_topo

STEP = [1, 2, 3]
C = 448
CA = 320
BF, F32, I32, U16, MX, U8 = "bfloat16", "float32", "int32", "uint16", "float8_e4m3fn_x4", "uint8"

SCRATCH = {}
for _n, _w in (("x0", 1792), ("xt", 1792), ("xh", 1792), ("xg", 1792), ("vt", 1792), ("ht", 1792), ("dd", 1792), ("ut", 512), ("vv", 512),
               ("wt", 1408), ("eb", 2048), ("zt", 848), ("ident", 128), ("jcol", 128),
               ("iot", C), ("j16", C), ("j4", C), ("mask16", C), ("mask4", C), ("seg16", C), ("seg4", C), ("masku", 112),
               ("mf0", C), ("mf1", C), ("mb0", C), ("mb1", C), ("rowq", C), ("rowm", C), ("rowqi", C), ("wA", C), ("wB", C),
               ("mg", C), ("sc", C), ("sc4", C), ("pu", 112), ("pus", 112), ("nu", C), ("sg", C), ("tab", 16), ("pa", 28), ("ag", 28)):
    SCRATCH[_n] = ("sbuf", [128, _w], BF)
for _n, _w in (("uc", 128), ("uq", 128), ("vq", 128), ("wq", 512), ("xc", C), ("vc", C), ("ebc", 512), ("shc", 352), ("zc", 212),
               ("hc0", C), ("hc1", C), ("hc2", C), ("lc0", C), ("lc1", C), ("lc2", C)):
    SCRATCH[_n] = ("sbuf", [128, _w], MX)
    SCRATCH[_n + "p"] = ("sbuf", [128, _w], U8)
for _n, _w in (("qU", 28), ("mU", 28), ("loU", 28), ("qiU", 28), ("loqU", 28), ("lf", 224), ("lb", 224), ("l4", 112), ("p16", 28),
               ("a8", 28), ("loP", 28), ("loqP", 28), ("dU", 28), ("ulist", 8), ("qoU", 28)):
    SCRATCH[_n] = ("sbuf", [128, _w], U16)
for _n, _w in (("iwb", 224), ("iw", 28), ("qF", 224), ("dF", 224), ("qB", 224), ("dB", 224), ("t1", 112), ("t2", 112), ("t3", 28), ("t4", 28),
               ("mF", 28), ("t5", 28), ("t6", 28), ("t7", 28), ("t8", 28), ("t9", 28), ("lo", 28), ("loq", 28), ("dhF", 28), ("qhF", 28), ("dhB", 28), ("qhB", 28), ("cp", 1), ("cp16", 1), ("cphi", 1), ("cq", 4), ("ysb", C), ("qrow", C)):
    SCRATCH[_n] = ("sbuf", [128, _w], F32)
for _n, _w in (("gqi", 28), ("gmi", 28), ("li", 84), ("pi", 4), ("uli", 16)):
    SCRATCH[_n] = ("sbuf", [128, _w], I32)
SCRATCH["dl"] = ("dram", [32, 4, 28], U16)
for _k in range(8):
    SCRATCH["P%d" % _k] = ("psum", [128, 512], F32)
SEMAPHORES = ["v", "s", "t", "gc"] + ["d%d" % k for k in range(40)] + ["arr%d" % k for k in range(3)] + ["snt%d" % k for k in range(3)]


def rank_program(g, core, T, topo):
    rank = T.rank_of(core)
    if rank is None:
        return
    A = AluOpType
    F = ActivationFunctionType
    queue = {"v": g.vector, "s": g.scalar, "t": g.tensor, "g": g, "y": g.sync}
    own = {"v": "v", "s": "s", "t": "t", "g": "gc"}
    known = {q: {} for q in queue}
    count, W, R, nd = {}, {}, {}, [0]

    def need(q, toks):
        best = {}
        for tok in toks:
            if tok[0] not in best or best[tok[0]][1] < tok[1]:
                best[tok[0]] = tok
        order = sorted(best.values(), key=lambda k: -len(k[2]))
        for sem, val, snap in order:
            if known[q].get(sem, 0) < val:
                queue[q].wait_ge(T.sem[sem], val)
                known[q][sem] = val
            for k, x in snap.items():
                if known[q].get(k, 0) < x:
                    known[q][k] = x

    def deps(reads, writes):
        toks = []
        for k in reads:
            toks += W[k]
        for k in writes:
            toks += W.get(k, []) + list(R.get(k, {}).values())
        return toks

    def done(tok, reads, writes):
        for k in writes:
            W[k] = [tok]
            R[k] = {}
        for k in reads:
            if k not in writes:
                R.setdefault(k, {})[tok[0]] = tok

    def op(q, reads, writes, call):
        need(q, deps(reads, writes))
        sem = own[q]
        count[sem] = count.get(sem, 0) + 1
        call().then_inc(T.sem[sem], 1)
        done((sem, count[sem], dict(known[q])), reads, writes)

    def dma(q, pairs, reads, writes):
        need(q, deps(reads, writes))
        sem = "d%d" % nd[0]
        nd[0] += 1
        for o, i in pairs:
            queue[q].dma_start(o, i).then_inc(T.sem[sem], 16)
        count[sem] = 16 * len(pairs)
        done((sem, count[sem], dict(known[q])), reads, writes)

    def tt(reads, writes, out, a, b, o):
        op("v", reads, writes, lambda: g.vector.tensor_tensor(out, a, b, o))

    def ts(reads, writes, out, a, s1, o1, s2=None, o2=None):
        if o2 is None:
            op("v", reads, writes, lambda: g.vector.tensor_scalar(out, a, s1, None, o1))
        else:
            op("v", reads, writes, lambda: g.vector.tensor_scalar(out, a, s1, s2, o1, o2))

    def cp(reads, writes, out, a):
        op("v", reads, writes, lambda: g.vector.tensor_copy(out, a))

    def fill(writes, out, c):
        op("v", [], writes, lambda: g.vector.memset(out, c))

    def act(reads, writes, out, a, f=F.Copy, **kw):
        op("s", reads, writes, lambda: g.scalar.activation(out, a, f, **kw))

    def quant(reads, writes, c, a, b, src, e):
        op("v", reads, writes, lambda: g.vector.quantize_mx(T[c][:, a:b], T[c + "p"][:, a:b], src[:, e:e + 4 * (b - a)]))

    def mm(reads, writes, out, w, wa, x, xa, n):
        op("t", reads, writes, lambda: g.tensor.matmul_mx(out, T[w][:, wa:wa + 128], T[w + "p"][:, wa:wa + 128], T[x][:, xa:xa + n], T[x + "p"][:, xa:xa + n], True, True))

    def scan(reads, writes, out, seg, a):
        op("v", reads, writes, lambda: g.vector.tensor_tensor_scan(out, seg, a, 0.0, A.mult, A.add))

    dma("y", [(T.gqi[:], T.gq[:])], [], ["gqi"])
    dma("y", [(T.gmi[:], T.gm[:])], [], ["gmi"])
    dma("y", [(T.ut[:], T.u[:])], [], ["ut"])
    dma("s", [(T.x0[:, 0:4 * CA], T.x[:, 0:4 * CA])], [], ["x0A"])
    dma("s", [(T.x0[:, 4 * CA:], T.x[:, 4 * CA:])], [], ["x0B"])
    dma("y", [(T.vv[:], T.v[:])], [], ["vv"])
    dma("y", [(T.wq[:].bitcast(dt.uint8), T.wc[:])], [], ["wqc"])
    dma("y", [(T.wqp[:], T.ws[:])], [], ["wqp"])

    def iota(key, out, pat, base, cm, flag=True):
        if flag:
            op("g", [], [key], lambda: g.iota(out, pat, base, cm, allow_small_or_imprecise_dtypes=True))
        else:
            op("g", [], [key], lambda: g.iota(out, pat, base, cm))
    iota("pi", T.pi[:, 0:1], [[0, 1]], 0, 1, False)
    iota("uli", T.uli[:, 0:8], [[16, 8]], -16, 0, False)
    iota("j16", T.j16[:], [[0, 28], [1, 16]], 0, 0)
    iota("jcol", T.jcol[:], [[1, 128]], 0, 0)
    iota("iot", T.iot[:], [[1, C]], -224, 0)
    iota("iwb", T.iwb[:], [[0, 8], [16, 28]], 0, 0)
    iota("j4", T.j4[:], [[0, 112], [1, 4]], 0, 0)
    cplo, c896, cpt, cpp = (T.cq[:, k:k + 1] for k in range(4))
    ts(["pi"], ["pi1"], T.pi[:, 1:2], T.pi[:, 0:1], 15, A.bitwise_and)
    ts(["pi"], ["pi2"], T.pi[:, 2:3], T.pi[:, 0:1], 2, A.arith_shift_right, 3, A.bitwise_and)
    ts(["pi"], ["pi3"], T.pi[:, 3:4], T.pi[:, 0:1], 3, A.bitwise_and)
    ts(["uli"], ["uli2"], T.uli[:, 8:16], T.uli[:, 0:8], 127, A.bitwise_and)
    cp(["pi"], ["cp"], T.cp[:], T.pi[:, 0:1])
    cp(["pi1"], ["cp16"], T.cp16[:], T.pi[:, 1:2])
    cp(["pi2"], ["cphi"], T.cphi[:], T.pi[:, 2:3])
    cp(["pi3"], ["cplo"], cplo, T.pi[:, 3:4])
    cp(["uli2"], ["ulist"], T.ulist[:], T.uli[:, 8:16])
    ts(["cplo"], ["c896"], c896, cplo, 896.0, A.add)
    ts(["cplo"], ["cpt"], cpt, cplo, 4.0, A.mult, -224.0, A.add)
    fill(["zt"], T.zt[:], 0.0)
    fill(["wt"], T.wt[:], 0.0)
    ts(["j16", "cp16"], ["mask16"], T.mask16[:], T.j16[:], T.cp16[:], A.is_equal)
    ts(["j16"], ["seg16"], T.seg16[:], T.j16[:], 0.0, A.is_gt)
    ts(["jcol", "cp"], ["ident"], T.ident[:], T.jcol[:], T.cp[:], A.is_equal)
    ts(["jcol"], ["tab"], T.tab[:], T.jcol[:, 0:16], -2.0, A.mult, 1.0, A.add)
    cp(["ident"], ["wt"], T.wt[:, 448:960:4], T.ident[:])
    quant(["wt"], ["shc"], "shc", 0, 352, T.wt, 0)
    quant(["zt"], ["zcr"], "zc", 84, 212, T.zt, 336)
    ts(["iwb", "cp16"], ["iw"], T.iw[:], T.iwb[:, 0:28], T.cp16[:], A.add)
    ts(["iwb", "cp16"], ["qF0", "qFr"], T.qF[:], T.iwb[:], T.cp16[:], A.add)
    fill(["dF0", "dFr"], T.dF[:], 0.0)

    cp(["gqi"], ["qU"], T.qU[:], T.gqi[:])
    act(["iot", "qU"], ["rowq"], T.rowq[:], T.iot[:, 0:C].indirect(T.qU[:, 0:28]))
    cp(["gqi"], ["qF0"], T.qF[:, 0:28], T.gqi[:])
    cp(["gmi"], ["mU"], T.mU[:], T.gmi[:])
    cp(["gmi"], ["mF"], T.mF[:], T.gmi[:])
    dma("y", [(T.qF[16 * n:128, 28 * n:28 * n + 28], T.qF[0:128 - 16 * n, 0:28]) for n in range(1, 8)], ["qF0"], ["qFr"])
    tt(["mF", "iw"], ["lo"], T.lo[:], T.mF[:], T.iw[:], A.min)
    quant(["ut"], ["uc"], "uc", 0, 128, T.ut, 0)
    cp(["lo"], ["loU"], T.loU[:], T.lo[:])
    tt(["rowq", "mU", "mask16"], ["mg"], T.mg[:], T.rowq[:, 0:C].indirect(T.mU[:, 0:28]), T.mask16[:], A.mult)
    scan(["seg16", "mg"], ["sc"], T.sc[:], T.seg16[:], T.mg[:])
    ts(["sc"], ["t6"], T.t6[:], T.sc[:, 15:C:16], 224.0, A.add)
    tt(["t6", "qF0"], ["dF0"], T.dF[:, 0:28], T.t6[:], T.qF[:, 0:28], A.subtract)
    dma("y", [(T.dF[16 * n:128, 28 * n:28 * n + 28], T.dF[0:128 - 16 * n, 0:28]) for n in range(1, 8)], ["dF0"], ["dFr"])
    for a, b in ((0, 848), (848, 1696), (1696, 2048)):
        act(["zt"], ["eb%d" % a], T.eb[:, a:b], T.zt[:, 0:b - a])
    for b in range(4):
        act(["ident", "eb0", "eb848", "eb1696"], ["ebi%d" % b], T.eb[:, 512 * b + b:512 * b + 512:4], T.ident[:])
    cp(["uc", "ulist"], ["uqc"], T.uq[:, 0:128].bitcast(dt.uint32), T.uc[:, 0:128].bitcast(dt.uint32).indirect(T.ulist[:, 0:8]))
    cp(["uc", "ulist"], ["uqs"], T.uqp[:, 0:128], T.ucp[:, 0:128].indirect(T.ulist[:, 0:8]))

    def score(src, key, c, part):
        a, b, bank = (0, CA, "P0") if part == "A" else (CA, C, "P3")
        quant([key + part], [c + part], c, a, b, src, 4 * a)
        mm(["uqc", "uqs", c + part], [bank], T[bank][:, 0:b - a], "uq", 0, c, a, b - a)

    def sign(part):
        a, b, bank = (0, CA, "P0") if part == "A" else (CA, C, "P3")
        act([bank], ["sg" + part], T.sg[:, a:b], T[bank][:, 0:b - a], F.Sign, bias=-(2.0 ** -93))

    def halve(src, key, a, b, piece):
        act([key], ["xh%d" % piece], T.xh[:, a:b], src[:, a:b], F.Copy, scale=0.5)

    XH = ["xh0", "xh1", "xh2"]
    score(T.x0, "x0", "xc", "A")
    score(T.x0, "x0", "xc", "B")
    sign("A")
    sign("B")
    quant(["vv"], ["vq"], "vq", 0, 128, T.vv, 0)
    ts(["dF0"], ["dhF"], T.dhF[:], T.dF[:, 0:28], 0.5, A.mult)
    tt(["dhF", "qF0"], ["qhF"], T.qhF[:], T.dhF[:], T.qF[:, 0:28], A.add)
    quant(["ebi0", "ebi1", "ebi2", "ebi3"], ["ebc"], "ebc", 0, 512, T.eb, 0)
    halve(T.x0, "x0A", 0, 512, 0)
    halve(T.x0, "x0A", 512, 4 * CA, 1)
    halve(T.x0, "x0B", 4 * CA, 4 * C, 2)
    tt(["cpt", "cphi"], ["cpp"], cpp, cpt, T.cphi[:], A.add)

    def late_constants():
        ts(["j4", "cphi"], ["mask4"], T.mask4[:], T.j4[:], T.cphi[:], A.is_equal)
        ts(["j4"], ["seg4"], T.seg4[:], T.j4[:], 0.0, A.is_gt)
        ts(["j4", "cplo"], ["masku"], T.masku[:], T.j4[:, 0:112], cplo, A.is_equal)
        ts(["iwb", "cpp"], ["ag0", "ag"], T.ag[:], T.iwb[:, 0:28], cpp, A.add)

    def turned(src, dst):
        cp([src], ["li"], T.li[:, 0:28], T[src][:])
        ts(["li"], ["li1"], T.li[:, 28:56], T.li[:, 0:28], 3, A.bitwise_and)
        ts(["li"], ["li2"], T.li[:, 56:84], T.li[:, 0:28], 2, A.arith_shift_right, 3, A.bitwise_and)
        tt(["li1", "li2"], ["t9"], T.t9[:], T.li[:, 28:56], T.li[:, 56:84], A.subtract)
        ts(["t9"], ["t5"], T.t5[:], T.t9[:], 3.0, A.mult)
        tt(["t5", src], ["t6"], T.t6[:], T.t5[:], T[src][:], A.add)
        cp(["t6"], [dst], T[dst][:], T.t6[:])

    def back_tables_1():
        cp(["iot", "qU"], ["rowqi"], T.rowqi[:, 0:C].indirect(T.qU[:, 0:28]), T.iot[:])

    def back_tables_2():
        tt(["rowqi", "mask16"], ["mg"], T.mg[:], T.rowqi[:], T.mask16[:], A.mult)
        scan(["seg16", "mg"], ["sc"], T.sc[:], T.seg16[:], T.mg[:])
        ts(["sc"], ["qiU"], T.qiU[:], T.sc[:, 15:C:16], 224.0, A.add)
        ts(["sc"], ["qB0"], T.qB[:, 0:28], T.sc[:, 15:C:16], 224.0, A.add)
        dma("y", [(T.qB[0:128 - 16 * n, 28 * n:28 * n + 28], T.qB[16 * n:128, 0:28]) for n in range(1, 8)], ["qB0"], ["qBr"])
        tt(["rowm", "qiU", "mask16"], ["mg"], T.mg[:], T.rowm[:, 0:C].indirect(T.qiU[:, 0:28]), T.mask16[:], A.mult)
        scan(["seg16", "mg"], ["sc"], T.sc[:], T.seg16[:], T.mg[:])
        ts(["sc"], ["t7"], T.t7[:], T.sc[:, 15:C:16], 224.0, A.add)
        tt(["t7", "qB0"], ["dB0"], T.dB[:, 0:28], T.t7[:], T.qB[:, 0:28], A.subtract)
        dma("y", [(T.dB[0:128 - 16 * n, 28 * n:28 * n + 28], T.dB[16 * n:128, 0:28]) for n in range(1, 8)], ["dB0"], ["dBr"])
        tt(["t7", "qB0"], ["loq"], T.loq[:], T.t7[:], T.qB[:, 0:28], A.min)
        ts(["dB0"], ["dhB"], T.dhB[:], T.dB[:, 0:28], 0.5, A.mult)
        cp(["loq"], ["loqU"], T.loqU[:], T.loq[:])
        tt(["dhB", "qB0"], ["qhB"], T.qhB[:], T.dhB[:], T.qB[:, 0:28], A.add)

    def spread(lo, mask, lst, q, d, way):
        tt(["sgA", "sgB", lo, mask], ["mg"], T.mg[:], T.sg[:, 0:C].indirect(T[lo][:, 0:28]), T[mask][:], A.mult)
        scan(["seg16", "mg"], ["sc"], T.sc[:], T.seg16[:], T.mg[:])
        dh, qh = ("dhF", "qhF") if lst == "lf" else ("dhB", "qhB")
        ts(["sc"], ["zt"], T.zt[:, 336:448:4], T.sc[:, 15:C:16], 0.0, A.is_gt)
        tt(["sc", dh], ["t3"], T.t3[:], T.sc[:, 15:C:16], T[dh][:], A.mult)
        quant(["zt"], ["zc"], "zc", 0, 128, T.zt, 0)
        tt(["t3", qh], ["t4"], T.t4[:], T.t3[:], T[qh][:], A.add)
        cp(["t4"], [lst + "o"], T[lst][:, 0:28], T.t4[:])
        for bank, ns in (("P1", (1, 2, 3)), ("P2", (4, 5, 6, 7))):
            need("t", deps(["zc", "zcr", "shc"], [bank]))
            for n in ns:
                s0, z0 = 112 + way * 16 * n, 84 - 28 * (n - ns[0])
                i = g.tensor.matmul_mx(T[bank][:, 0:128], T.shc[:, s0:s0 + 128], T.shcp[:, s0:s0 + 128], T.zc[:, z0:z0 + 128], T.zcp[:, z0:z0 + 128], n == ns[0], n == ns[-1])
            count["t"] = count.get("t", 0) + 1
            i.then_inc(T.sem["t"], 1)
            done(("t", count["t"], dict(known["t"])), ["zc", "zcr", "shc"], [bank])

    def prep(k, part, lst, q, d):
        bank, a, n = ("P1", 28, 84) if part == "A" else ("P2", 112, 112)
        if k == 0:
            tt([bank, d + "r"], ["t1"], T.t1[:, 0:n], T[bank][:, 0:n], T[d][:, a:a + n], A.mult)
        if k == 1:
            tt(["t1", q + "r"], ["t2"], T.t2[:, 0:n], T.t1[:, 0:n], T[q][:, a:a + n], A.add)
        if k == 2:
            cp(["t2"], [lst + part], T[lst][:, a:a + n], T.t2[:, 0:n])

    def gather(i, lst, nv):
        src = "iot" if i == 0 else ("wB", "wA")[i % 2]
        dst = ("wA", "wB")[i % 2]
        key = ["iot"] if i == 0 else [src + "v", src + "s"]
        lk = lst + ("o" if i == 0 else "A" if i < 4 else "B")
        if nv:
            cp(key + [lk], [dst + "v"] + ([dst + "s"] if nv == 28 else []), T[dst][:, 0:16 * nv], T[src][:, 0:C].indirect(T[lst][:, 28 * i:28 * i + nv]))
        if nv < 28:
            act(key + [lk], [dst + "s"] + ([dst + "v"] if nv == 0 else []), T[dst][:, 16 * nv:C], T[src][:, 0:C].indirect(T[lst][:, 28 * i + nv:28 * i + 28]))

    def offsets(src, off, offkeys):
        tt([src + "v", src + "s", "mask4"] + offkeys, ["mg"], T.mg[:], T[src][:, 0:C].indirect(off), T.mask4[:], A.mult)
        scan(["seg4", "mg"], ["sc4"], T.sc4[:], T.seg4[:], T.mg[:])
        ts(["sc4", "c896"], ["l4"], T.l4[:], T.sc4[:, 3:C:4], 4.0, A.mult, c896, A.add)

    def move(out, okey, win, wkeys, base, bkeys, part):
        a, b = (0, CA) if part == "A" else (CA, C)
        tt(wkeys + ["l4"] + bkeys, [okey + part], out[:, 4 * a:4 * b], win[:, 0:4 * C].indirect(T.l4[:, a // 4:b // 4]), base[:, 4 * a:4 * b], A.add)

    mf, mb = "mask16", "mask16"
    for r in range(3):
        dst = T.cores[rank ^ STEP[r]]
        hc, lc = "hc%d" % r, "lc%d" % r
        dma("y", [(T.xg[:], T.xh[:])], XH, ["xg"])
        spread("loU", mf, "lf", "qF", "dF", -1)
        gather(0, "lf", 0 if r == 0 else 4)
        for k in range(3):
            prep(k, "A", "lf", "qF", "dF")
        if r == 0:
            for k in range(3):
                prep(k, "B", "lf", "qF", "dF")
            for k in range(1, 7):
                gather(k, "lf", 0)
                if k == 2:
                    act(["iwb", "cp16"], ["qB0", "qBr"], T.qB[:], T.iwb[:], F.Identity, bias=T.cp16[:])
                    act(["wt"], ["dB0", "dBr"], T.dB[:], T.wt[:, 0:224])
                    act(["iot", "mU"], ["rowm"], T.rowm[:], T.iot[:, 0:C].indirect(T.mU[:, 0:28]))
            late_constants()
            back_tables_1()
            back_tables_2()
        else:
            gather(1, "lf", 10)
            prep(0, "B", "lf", "qF", "dF")
            gather(2, "lf", 8)
            prep(1, "B", "lf", "qF", "dF")
            gather(3, "lf", 10)
            prep(2, "B", "lf", "qF", "dF")
            gather(4, "lf", 0)
            nxt = "mb%d" % (r % 2)
            tt(["nu", "loqP", mb], [nxt], T[nxt][:], T.nu[:, 0:C].indirect(T.loqP[:, 0:28]), T[mb][:], A.mult)
            mb = nxt
            gather(5, "lf", 14)
            gather(6, "lf", 14)
        offsets("wA", T.lf[:, 196:224], ["lfB"])
        move(T.vt, "vt", T.xh, XH, T.xg, ["xg"], "A")
        score(T.vt, "vt", "vc", "A")
        sign("A")

        def layer(b, part):
            a, e = (0, CA) if part == "A" else (CA, C)
            bank = "P%d" % (4 + b)
            mm(["wqc", "wqp", "vc" + part], [bank], T[bank][:, 0:e - a], "wq", 128 * b, "vc", a, e - a)
            act([bank], ["ht%d%s" % (b, part)], T.ht[:, 4 * a + b:4 * e:4], T[bank][:, 0:e - a], F.Copy, scale=0.03125)
        layer(0, "A")
        move(T.vt, "vt", T.xh, XH, T.xg, ["xg"], "B")
        mm(["wqc", "wqp", "vcA"], ["P5"], T.P5[:, 0:CA], "wq", 128, "vc", 0, CA)
        score(T.vt, "vt", "vc", "B")
        sign("B")
        act(["P5"], ["ht1A"], T.ht[:, 1:4 * CA:4], T.P5[:, 0:CA], F.Copy, scale=0.03125)
        layer(2, "A")
        layer(3, "A")
        for b in range(4):
            layer(b, "B")
        tt(["sc4", "masku"], ["pu"], T.pu[:], T.sc4[:, 3:C:4], T.masku[:], A.mult)
        scan(["seg4", "pu"], ["pus"], T.pus[:], T.seg4[:, 0:112], T.pu[:])
        ts(["pus"], ["p16"], T.p16[:], T.pus[:, 3:112:4], 224.0, A.add)
        cp(["pus"], ["pa"], T.pa[:], T.pus[:, 3:112:4])
        dma("y", [(T.dl[k:32:4, :, :], T.p16[k:128:4, :]) for k in range(4)], ["p16"], ["dl"])
        dma("y", [(T.ag[16:128, :], T.pa[0:112, :])], ["pa"], ["ag"])
        dma("y", [(T.a8[16 * k:16 * k + 16, :], T.dl[28:32, :, :]) for k in range(8)], ["dl"], ["a8"])
        spread("loqU", mb, "lb", "qB", "dB", 1)
        quant(["ht%d%s" % (b, k) for b in range(4) for k in "AB"], [hc], hc, 0, C, T.ht, 0)
        need("g", W[hc])
        rid, pid, _ = topo.addr(dst)
        mask, ne = topo.mask(core, dst), len(topo.engines(core, dst))
        arr, snt = "arr%d" % r, "snt%d" % r
        g.remote_dma(out_ap=T[lc][:, 0:C].bitcast(dt.uint8), in_ap=T[hc][:, 0:C].bitcast(dt.uint8), remote_sem=T.sem[arr], local_sem=T.sem[snt], pid=pid, routing_id=rid, dma_engine_mask=mask)
        g.remote_dma(out_ap=T[lc + "p"][:, 0:C], in_ap=T[hc + "p"][:, 0:C], remote_sem=T.sem[arr], local_sem=T.sem[snt], pid=pid, routing_id=rid, dma_engine_mask=mask)
        count[arr] = count[snt] = 2 * ne
        W[lc] = [(arr, 2 * ne, {})]
        gather(0, "lb", 0)
        for k in range(3):
            prep(k, "A", "lb", "qB", "dB")
        gather(1, "lb", 10)
        prep(0, "B", "lb", "qB", "dB")
        gather(2, "lb", 8)
        prep(1, "B", "lb", "qB", "dB")
        gather(3, "lb", 10)
        prep(2, "B", "lb", "qB", "dB")
        gather(4, "lb", 14)
        gather(5, "lb", 14)
        gather(6, "lb", 28)
        gather(7, "lb", 28)
        for b in range(4):
            bank = "P%d" % (4 + b)
            mm(["ebc", lc], [bank], T[bank][:, 0:C], "ebc", 128 * b, lc, 0, C)
            act([bank], ["dd%d" % b], T.dd[:, b:4 * C:4], T[bank][:, 0:C])
        offsets("wB", T.a8[:, 0:28], ["a8"])
        tt(["sc4", "masku"], ["pu"], T.pu[:], T.sc4[:, 3:C:4], T.masku[:], A.mult)
        scan(["seg4", "pu"], ["pus"], T.pus[:], T.seg4[:, 0:112], T.pu[:])
        if r == 0:
            turned("lo", "loP")
            turned("loq", "loqP")

        def differ(k):
            if k == 0:
                tt(["pus", "ag", "ag0"], ["t8"], T.t8[:], T.pus[:, 3:112:4], T.ag[:], A.subtract)
            else:
                ts(["t8"], ["dU"], T.dU[:], T.t8[:], 0.0, A.not_equal)
                act(["tab", "dU"], ["nu"], T.nu[:], T.tab[:, 0:16].indirect(T.dU[:, 0:28]))

        def turn(old):
            new = "mf%d" % (r % 2)
            tt(["nu", "loP", old], [new], T[new][:], T.nu[:, 0:C].indirect(T.loP[:, 0:28]), T[old][:], A.mult)
            return new
        DD = ["dd%d" % b for b in range(4)]
        if r < 2:
            move(T.xt, "xt", T.dd, DD, T.vt, ["vtA"], "A")
            differ(0)
            score(T.xt, "xt", "xc", "A")
            differ(1)
            move(T.xt, "xt", T.dd, DD, T.vt, ["vtB"], "B")
            score(T.xt, "xt", "xc", "B")
            sign("A")
            halve(T.xt, "xtA", 0, 512, 0)
            sign("B")
            halve(T.xt, "xtA", 512, 4 * CA, 1)
            halve(T.xt, "xtB", 4 * CA, 4 * C, 2)
            mf = turn(mf)
        else:
            differ(0)
            differ(1)
            for part, bank, a, b in (("A", "P0", 0, CA), ("B", "P3", CA, C)):
                move(T.xt, "xt", T.dd, DD, T.vt, ["vt" + part], part)
                if part == "A":
                    mf = turn(mf)
                    scan(["seg16", mf], ["sc"], T.sc[:], T.seg16[:], T[mf][:])
                    ts(["sc"], ["t3"], T.t3[:], T.sc[:, 15:C:16], 0.0, A.is_lt)
                    tt(["t3", "dF0"], ["t5"], T.t5[:], T.t3[:], T.dF[:, 0:28], A.mult)
                    tt(["t5", "qF0"], ["t6"], T.t6[:], T.t5[:], T.qF[:, 0:28], A.add)
                    cp(["t6"], ["qoU"], T.qoU[:], T.t6[:])
                    act(["iot", "qoU"], ["qrow"], T.qrow[:], T.iot[:, 0:C].indirect(T.qoU[:, 0:28]), F.Identity, bias=224.0)
                    dma("y", [(T.qo[:], T.qrow[0:128:16, :])], ["qrow"], ["qo"])
                quant(["xt" + part], ["xc" + part], "xc", a, b, T.xt, 4 * a)
                mm(["vq", "xc" + part], [bank], T[bank][:, 0:b - a], "vq", 0, "xc", a, b - a)
                act([bank], ["y" + part], T.ysb[:, a:b], T[bank][:, 0:b - a])
                dma("s", [(T.y[:, a:b], T.ysb[:, a:b])], ["y" + part], ["yo" + part])
                dma("y", [(T.oc[:, 4 * a:4 * b], T.xc[:, a:b].bitcast(dt.uint8))] + [(T.osc[4 * k:4 * k + 4, a:b], T.xcp[32 * k:32 * k + 4, a:b]) for k in range(4)], ["xc" + part], ["oo" + part])
    for sem in count:
        if known["g"].get(sem, 0) < count[sem]:
            g.wait_ge(T.sem[sem], count[sem])
